import numpy as np
import ml_dtypes


def mxq(x, axis, fmt="e4m3"):
    dtype, down = {"e4m3": (ml_dtypes.float8_e4m3fn, 7), "e5m2": (ml_dtypes.float8_e5m2, 14)}[fmt]
    v = np.moveaxis(np.asarray(x, np.float32).astype(ml_dtypes.bfloat16).astype(np.float64), axis, -1)
    blocks = v.reshape(v.shape[:-1] + (-1, 32))
    amax = np.abs(blocks).max(-1, keepdims=True)
    byte = np.maximum(np.where(amax > 0, np.frexp(amax)[1] - 1 + 127, 0) - down, 1)
    scale = np.exp2(byte - 127.0)
    codes = (blocks / scale).astype(np.float32).astype(dtype).astype(np.float64)
    return np.moveaxis((codes * scale).reshape(v.shape), -1, axis)


WIDE = False


def mx_kscale(k):
    if not WIDE:
        return np.ones(k)
    levels = np.array([10, -10, 5, -5, 0])
    if k % 512:
        return np.exp2(np.random.permutation(np.resize(levels, k // 32))).repeat(32)
    a = np.empty((k // 512, 16))
    for p in range(k // 512):
        a[p, :8] = np.random.permutation(np.resize(levels, 8))
        for g in range(8):
            far = levels[np.abs(levels - a[p, g]) >= 10]
            a[p, g + 8] = far[np.random.randint(len(far))]
    return np.exp2(a.ravel()).repeat(32)


def f64(x):
    return np.asarray(x).astype(np.float64)


def striped(idx):
    return np.tile(idx.reshape(-1, 16).T, (8, 1)).astype(np.uint16)


def unstriped(offs):
    return offs[:16].T.reshape(-1).astype(np.int64)


def pack_weight(w):
    k, n = w.shape
    w = f64(np.asarray(w, np.float32).astype(ml_dtypes.bfloat16)).reshape(k // 32, 32, n)
    amax = np.abs(w).max(1)
    byte = np.clip(np.where(amax > 0, np.frexp(amax)[1] - 1 + 127 - 7, 1), 1, 254)
    scaled = (w * np.exp2(127.0 - byte)[:, None, :]).reshape(k, n).astype(np.float32)
    words = np.ascontiguousarray(scaled.reshape(k // 512, 128, 4, n).transpose(0, 1, 3, 2)).astype(ml_dtypes.float8_e4m3fn).view(np.uint8)
    return words, np.ascontiguousarray(byte.astype(np.uint8).reshape(k // 512, 16, n))


def unpack_weight(words, scales):
    g, p, n, _ = words.shape
    vals = np.ascontiguousarray(words).view(ml_dtypes.float8_e4m3fn).astype(np.float64) * np.repeat(np.exp2(scales.astype(np.float64) - 127.0), 8, axis=1)[..., None]
    return vals.transpose(0, 1, 3, 2).reshape(g * 512, n)


def planes(y):
    n, m = y.shape
    v = y.astype(np.float32).astype(ml_dtypes.bfloat16).astype(np.float64).reshape(n // 32, 32, m)
    top = np.abs(v).max(1)
    byte = np.clip(np.where(top > 0, np.frexp(top)[1] - 1 + 127 - 7, 1), 1, 254)
    codes = (v * np.exp2(127.0 - byte)[:, None, :]).reshape(n, m).astype(np.float32).astype(ml_dtypes.float8_e4m3fn).view(np.uint8)
    words = codes.reshape(n // 512, 128, 4, m).transpose(0, 1, 3, 2)
    return np.ascontiguousarray(words), np.ascontiguousarray(byte.astype(np.uint8).reshape(n // 512, 16, m))


K, T, S, V, N = 512, 2048, 512, 256, 512


def setup_inputs():
    n = np.random.standard_normal
    s = mx_kscale(K)[:, None]
    packed_xT = pack_weight(n((K, T)) * s)
    return {
        "x_words": packed_xT[0],
        "x_scales": packed_xT[1],
        "w1": (n((K, N)) / np.sqrt(K) / s).astype(np.float32),
        "rate": (np.random.uniform(0.1, 0.6, (N, 1))).astype(np.float32),
        "offs": striped(np.random.permutation(T)[:S]),
        "cen": striped(np.random.permutation(S)[:V]),
        "pos1": striped(np.random.permutation(S)[:V]),
        "pos2": striped(np.random.permutation(S)[:V]),
    }


def reference(x_words, x_scales, w1, rate, offs, cen, pos1, pos2):
    xq = unpack_weight(x_words, x_scales)[:, unstriped(offs)]
    h = mxq(f64(w1), 0, "e4m3").T @ xq
    hc = h[:, unstriped(cen)]
    d0 = h[:, unstriped(pos1)] - hc
    d1 = h[:, unstriped(pos2)] - hc
    ss = d0 / ((d0) ** 2 + 1.0) + d1 / ((d1) ** 2 + 1.0)
    out_0 = hc + f64(rate) * ss
    return (out_0,) + planes(out_0)

@@ -1,0 +1,173 @@
+from contextlib import ExitStack
+
+import concourse.mybir as mybir
+from concourse.masks import make_identity
+
+K, T, S, V, N = 512, 2048, 512, 256, 512
+FLOPS = 2 * K * S * N
+
+F32 = mybir.dt.float32
+BF16 = mybir.dt.bfloat16
+I32 = mybir.dt.int32
+U32 = mybir.dt.uint32
+U16 = mybir.dt.uint16
+U8 = mybir.dt.uint8
+FP8X4 = mybir.dt.float8_e4m3fn_x4
+ACT = mybir.ActivationFunctionType
+ALU = mybir.AluOpType
+
+P = 128
+PACK = 4
+HALF = S // 2
+
+
+def tile_picked_ypm_pm_po_kernel(tc, x_words, x_scales, w1, rate, offs, cen, pos1, pos2, out_0, out_1, out_2):
+    nc = tc.nc
+    with ExitStack() as ctx:
+        lists = ctx.enter_context(tc.tile_pool(name="lists", bufs=1))
+        sb = ctx.enter_context(tc.tile_pool(name="sb", bufs=1))
+        psum = ctx.enter_context(tc.psum_pool(name="psum", bufs=1))
+
+        offs_t = lists.tile([P, S // 16], U16, name="offs_t")
+        cen_t = lists.tile([P, V // 16], U16, name="cen_t")
+        pos_t = [lists.tile([P, V // 16], U16, name="pos%d" % i) for i in range(2)]
+
+        xs_all = sb.tile([P, T], U8, name="xs_all", align_bytes=64)
+        xw_all = sb.tile([P, T], I32, name="xw_all", align_bytes=64)
+        w_raw = sb.tile([P, PACK, N], F32, name="w_raw", align_bytes=64)
+        rate_t = sb.tile([P, PACK], F32, name="rate_t")
+        warm = sb.tile([P, 8], F32, name="warm")
+        warm2 = sb.tile([P, 8], F32, name="warm2")
+
+        nc.vector.memset(xs_all[:].bitcast(I32), 0)
+        nc.gpsimd.memset(warm[:], 1.0)
+        nc.scalar.activation(warm2[:], warm[:], ACT.Abs_reciprocal_sqrt)
+
+        ident = sb.tile([P, P], F32, name="ident", align_bytes=64)
+        make_identity(nc, ident[:])
+
+        nc.sync.dma_start(w_raw[:], w1.rearrange("(p j) n -> p j n", j=PACK))
+        for q in range(4):
+            nc.sync.dma_start(xs_all[32 * q : 32 * q + 4, :].bitcast(I32), x_scales[0, 4 * q : 4 * q + 4, :].bitcast(I32))
+        nc.sync.dma_start(offs_t[:], offs)
+        nc.sync.dma_start(xw_all[:], x_words[0].rearrange("p c r -> p (c r)").bitcast(I32))
+        nc.sync.dma_start(cen_t[:], cen)
+        nc.sync.dma_start(pos_t[0][:], pos1)
+        nc.sync.dma_start(pos_t[1][:], pos2)
+        nc.sync.dma_start(rate_t[:], rate.rearrange("(p t) o -> p (t o)", t=PACK))
+
+        xs = sb.tile([P, S], U8, name="xs", align_bytes=64)
+        nc.vector.tensor_copy(xs[:], xs_all[:].indirect(offs_t[:]))
+
+        w_bf = sb.tile([P, PACK, P, PACK], BF16, name="w_bf", align_bytes=64)
+        src = w_raw[:].rearrange("p j (m t) -> p m j t", t=PACK)
+        dst = w_bf[:].rearrange("p t m j -> p m j t")
+        nc.scalar.copy(dst[:, 0:48], src[:, 0:48])
+        nc.vector.tensor_copy(dst[:, 48:P], src[:, 48:P])
+        w_codes = sb.tile([P, N], U32, name="w_codes", align_bytes=64)
+        w_scales = sb.tile([P, N], U8, name="w_scales", align_bytes=64)
+        nc.vector.quantize_mx(out=w_codes[:].bitcast(FP8X4), scales=w_scales[:], in_=w_bf[:].rearrange("p t m j -> p (t m j)"))
+
+        xw = sb.tile([P, S], U32, name="xw", align_bytes=64)
+        for a in range(2):
+            nc.vector.tensor_copy(
+                xw[:, a * HALF : (a + 1) * HALF],
+                xw_all[:].bitcast(U32).indirect(offs_t[:, a * HALF // 16 : (a + 1) * HALF // 16]),
+            )
+
+        def product(t, cols, name):
+            acc = psum.tile([P, cols.stop - cols.start], F32, name="acc", tag=name)
+            nc.tensor.matmul_mx(
+                out=acc[:],
+                lhsT=w_codes[:, t * P : (t + 1) * P].bitcast(FP8X4),
+                lhsT_scale=w_scales[:, t * P : (t + 1) * P],
+                rhs=xw[:, cols].bitcast(FP8X4),
+                rhs_scale=xs[:, cols],
+                start=True,
+                stop=True,
+            )
+            return acc
+
+        h = [sb.tile([P, S], F32, name="h%d" % t) for t in range(PACK)]
+        first, second = slice(0, HALF), slice(HALF, S)
+        for t in range(2):
+            nc.scalar.copy(h[t][:, first], product(t, first, "bank%d" % (4 + t))[:])
+        nc.scalar.copy(h[0][:, second], product(0, second, "bank0")[:])
+        nc.vector.tensor_copy(h[1][:, second], product(1, second, "bank1")[:])
+        for t in range(2, PACK):
+            nc.scalar.copy(h[t][:], product(t, slice(0, S), "bank%d" % t)[:])
+
+        hc = sb.tile([P, PACK, V], F32, name="hc")
+        y = sb.tile([P, PACK, V], F32, name="y")
+        d = sb.tile([P, 2, V], F32, name="d")
+        work = [sb.tile([P, V], F32, name="work%d" % i) for i in range(2)]
+        damp_own = sb.tile([P, PACK + 1, V], F32, name="damp_own")
+        g = [sb.tile([P, 2, V], F32, name="g%d" % t) for t in range(PACK)]
+        last = PACK - 1
+        damp = {}
+        for t in range(PACK):
+            damp[t, 0] = y[:, t - 1, :] if t > 0 else damp_own[:, PACK, :]
+            damp[t, 1] = damp_own[:, t, :]
+        d_tr = {}
+        for t in range(PACK):
+            if t % 2 == 0:
+                banks = [psum.tile([P, 2, V], F32, name="d_tr", tag="bank%d" % (t + i)) for i in range(2)]
+                for u in (t, t + 1):
+                    nc.vector.tensor_copy(hc[:, u, :], h[u][:].indirect(cen_t[:]))
+            for i in range(2):
+                d_tr[t, i] = banks[i][:, t % 2, :]
+                nc.vector.tensor_tensor(d[:, i, :], h[t][:].indirect(pos_t[i][:]), hc[:, t, :], ALU.subtract)
+                for a in range(2):
+                    nc.tensor.transpose(d_tr[t, i][:, a * P : (a + 1) * P], d[:, i, a * P : (a + 1) * P], ident[:])
+            for i in range(2):
+                nc.scalar.activation(work[i][:], d_tr[t, i], ACT.Square)
+            for i in range(2):
+                nc.scalar.activation(work[i][:], work[i][:], ACT.Abs_reciprocal_sqrt, bias=1.0)
+            for i in range(2):
+                nc.scalar.activation(damp[t, i], work[i][:], ACT.Square)
+
+        out_rows = out_0.rearrange("(p t) v -> p t v", t=PACK)
+
+        def back(out, t, i, a):
+            nc.tensor.matmul(out, lhsT=g[t][:, i, a * P : (a + 1) * P], rhs=ident[:], is_transpose=True, start=(i == 0), stop=(i == 1))
+
+        def step(t, cols, total):
+            nc.vector.scalar_tensor_tensor(y[:, t, cols], total, rate_t[:, t : t + 1], hc[:, t, cols], ALU.mult, ALU.add)
+
+        sums = []
+        for t in range(PACK):
+            for i in range(2):
+                nc.vector.tensor_tensor(g[t][:, i, :], d_tr[t, i], damp[t, i], ALU.mult)
+            if t < last:
+                total = psum.tile([P, V], F32, name="total", tag="bank%d" % (5 + t))
+                for a in range(2):
+                    for i in range(2):
+                        back(total[:, a * P : (a + 1) * P], t, i, a)
+                sums.append(total)
+            else:
+                last_sums = [psum.tile([P, P], F32, name="total", tag=tag) for tag in ("bank4", "bank0")]
+                for i in range(2):
+                    for a in range(2):
+                        back(last_sums[a][:], t, i, a)
+            if t > 0:
+                step(t - 1, slice(0, V), sums[t - 1][:])
+                nc.sync.dma_start(out_rows[:, t - 1, :], y[:, t - 1, :])
+        for a in range(2):
+            step(last, slice(a * P, (a + 1) * P), last_sums[a][:])
+        nc.sync.dma_start(out_rows[:, last, :], y[:, last, :])
+
+        y_bf = sb.tile([P, V, PACK], BF16, name="y_bf", align_bytes=64)
+        ysrc = y[:].rearrange("p t (c i) -> p c t i", i=4)
+        ydst = y_bf[:].rearrange("p (c i) t -> p c t i", i=4)
+        nc.scalar.copy(ydst[:, :, 0:2, :], ysrc[:, :, 0:2, :])
+        for a in range(2):
+            nc.vector.tensor_copy(ydst[:, 32 * a : 32 * (a + 1), 2:4, :], ysrc[:, 32 * a : 32 * (a + 1), 2:4, :])
+        y_codes = sb.tile([P, V], U32, name="y_codes", align_bytes=64)
+        y_scales = sb.tile([P, V], U8, name="y_scales", align_bytes=64)
+        for a in range(2):
+            cols = slice(a * P, (a + 1) * P)
+            nc.vector.quantize_mx(out=y_codes[:, cols].bitcast(FP8X4), scales=y_scales[:, cols], in_=y_bf[:, cols, :].rearrange("p v t -> p (v t)"))
+        nc.scalar.dma_start(out_1[0].rearrange("p c r -> p (c r)").bitcast(I32), y_codes[:].bitcast(I32))
+        for q in range(4):
+            eng = nc.scalar if q == 3 else nc.sync
+            eng.dma_start(out_2[0, 4 * q : 4 * q + 4, :].bitcast(I32), y_scales[32 * q : 32 * q + 4, :].bitcast(I32))

@@ -1,7 +1,6 @@
 from contextlib import ExitStack
 
 import concourse.mybir as mybir
-from concourse.masks import make_identity
 
 K, T, S, V, N = 512, 2048, 512, 256, 512
 FLOPS = 2 * K * S * N
@@ -43,9 +42,6 @@ def tile_picked_ypm_pm_po_kernel(tc, x_words, x_scales, w1, rate, offs, cen, pos
         nc.gpsimd.memset(warm[:], 1.0)
         nc.scalar.activation(warm2[:], warm[:], ACT.Abs_reciprocal_sqrt)
 
-        ident = sb.tile([P, P], F32, name="ident", align_bytes=64)
-        make_identity(nc, ident[:])
-
         nc.sync.dma_start(w_raw[:], w1.rearrange("(p j) n -> p j n", j=PACK))
         for q in range(4):
             nc.sync.dma_start(xs_all[32 * q : 32 * q + 4, :].bitcast(I32), x_scales[0, 4 * q : 4 * q + 4, :].bitcast(I32))
@@ -62,8 +58,8 @@ def tile_picked_ypm_pm_po_kernel(tc, x_words, x_scales, w1, rate, offs, cen, pos
         w_bf = sb.tile([P, PACK, P, PACK], BF16, name="w_bf", align_bytes=64)
         src = w_raw[:].rearrange("p j (m t) -> p m j t", t=PACK)
         dst = w_bf[:].rearrange("p t m j -> p m j t")
-        nc.scalar.copy(dst[:, 0:48], src[:, 0:48])
-        nc.vector.tensor_copy(dst[:, 48:P], src[:, 48:P])
+        nc.scalar.copy(dst[:, 0:64], src[:, 0:64])
+        nc.vector.tensor_copy(dst[:, 64:P], src[:, 64:P])
         w_codes = sb.tile([P, N], U32, name="w_codes", align_bytes=64)
         w_scales = sb.tile([P, N], U8, name="w_scales", align_bytes=64)
         nc.vector.quantize_mx(out=w_codes[:].bitcast(FP8X4), scales=w_scales[:], in_=w_bf[:].rearrange("p t m j -> p (t m j)"))
@@ -76,7 +72,7 @@ def tile_picked_ypm_pm_po_kernel(tc, x_words, x_scales, w1, rate, offs, cen, pos
             )
 
         def product(t, cols, name):
-            acc = psum.tile([P, cols.stop - cols.start], F32, name="acc", tag=name)
+            acc = psum.tile([P, cols.stop - cols.start], F32, name=name)
             nc.tensor.matmul_mx(
                 out=acc[:],
                 lhsT=w_codes[:, t * P : (t + 1) * P].bitcast(FP8X4),
@@ -89,77 +85,65 @@ def tile_picked_ypm_pm_po_kernel(tc, x_words, x_scales, w1, rate, offs, cen, pos
             return acc
 
         h = [sb.tile([P, S], F32, name="h%d" % t) for t in range(PACK)]
-        first, second = slice(0, HALF), slice(HALF, S)
-        for t in range(2):
-            nc.scalar.copy(h[t][:, first], product(t, first, "bank%d" % (4 + t))[:])
-        nc.scalar.copy(h[0][:, second], product(0, second, "bank0")[:])
-        nc.vector.tensor_copy(h[1][:, second], product(1, second, "bank1")[:])
-        for t in range(2, PACK):
-            nc.scalar.copy(h[t][:], product(t, slice(0, S), "bank%d" % t)[:])
+        halves = [slice(0, HALF), slice(HALF, S)]
+        for a, cols in enumerate(halves):
+            for t in range(2):
+                nc.scalar.copy(h[t][:, cols], product(t, cols, "acc%d_%d" % (t, a))[:])
+        accs = {t: product(t, slice(0, S), "acc%d" % t) for t in range(2, PACK)}
+        for cols in halves:
+            for t in range(2, PACK):
+                nc.scalar.copy(h[t][:, cols], accs[t][:, cols])
 
         hc = sb.tile([P, PACK, V], F32, name="hc")
         y = sb.tile([P, PACK, V], F32, name="y")
-        d = sb.tile([P, 2, V], F32, name="d")
-        work = [sb.tile([P, V], F32, name="work%d" % i) for i in range(2)]
-        damp_own = sb.tile([P, PACK + 1, V], F32, name="damp_own")
-        g = [sb.tile([P, 2, V], F32, name="g%d" % t) for t in range(PACK)]
-        last = PACK - 1
-        damp = {}
-        for t in range(PACK):
-            damp[t, 0] = y[:, t - 1, :] if t > 0 else damp_own[:, PACK, :]
-            damp[t, 1] = damp_own[:, t, :]
-        d_tr = {}
-        for t in range(PACK):
-            if t % 2 == 0:
-                banks = [psum.tile([P, 2, V], F32, name="d_tr", tag="bank%d" % (t + i)) for i in range(2)]
-                for u in (t, t + 1):
-                    nc.vector.tensor_copy(hc[:, u, :], h[u][:].indirect(cen_t[:]))
-            for i in range(2):
-                d_tr[t, i] = banks[i][:, t % 2, :]
-                nc.vector.tensor_tensor(d[:, i, :], h[t][:].indirect(pos_t[i][:]), hc[:, t, :], ALU.subtract)
-                for a in range(2):
-                    nc.tensor.transpose(d_tr[t, i][:, a * P : (a + 1) * P], d[:, i, a * P : (a + 1) * P], ident[:])
-            for i in range(2):
-                nc.scalar.activation(work[i][:], d_tr[t, i], ACT.Square)
-            for i in range(2):
-                nc.scalar.activation(work[i][:], work[i][:], ACT.Abs_reciprocal_sqrt, bias=1.0)
-            for i in range(2):
-                nc.scalar.activation(damp[t, i], work[i][:], ACT.Square)
+        d = [sb.tile([P, 2, V], F32, name="d%d" % t) for t in range(PACK)]
+        work = [sb.tile([P, 2, V], F32, name="work%d" % u) for u in range(2)]
+        damp = [sb.tile([P, 2, V], F32, name="damp%d" % t) for t in range(PACK)]
+        g = sb.tile([P, PACK, 2, V], F32, name="g")
+        part = sb.tile([P, PACK, V], F32, name="part")
+        pairs = [(0, 1), (2, 3)]
+        for pair in pairs:
+            for t in pair:
+                nc.vector.tensor_copy(hc[:, t, :], h[t][:].indirect(cen_t[:]))
+            for t in pair:
+                for i in range(2):
+                    nc.vector.tensor_tensor(d[t][:, i, :], h[t][:].indirect(pos_t[i][:]), hc[:, t, :], ALU.subtract)
+            for t in pair:
+                for i in range(2):
+                    nc.scalar.activation(work[t % 2][:, i, :], d[t][:, i, :], ACT.Square)
+            for t in pair:
+                nc.scalar.activation(work[t % 2][:], work[t % 2][:], ACT.Abs_reciprocal_sqrt, bias=1.0)
+            for t in pair:
+                nc.scalar.activation(damp[t][:], work[t % 2][:], ACT.Square)
 
         out_rows = out_0.rearrange("(p t) v -> p t v", t=PACK)
 
-        def back(out, t, i, a):
-            nc.tensor.matmul(out, lhsT=g[t][:, i, a * P : (a + 1) * P], rhs=ident[:], is_transpose=True, start=(i == 0), stop=(i == 1))
+        def pull(t, cols):
+            nc.vector.scalar_tensor_tensor(g[:, t, :, cols], d[t][:, :, cols], rate_t[:, t : t + 1], damp[t][:, :, cols], ALU.mult, ALU.mult)
 
-        def step(t, cols, total):
-            nc.vector.scalar_tensor_tensor(y[:, t, cols], total, rate_t[:, t : t + 1], hc[:, t, cols], ALU.mult, ALU.add)
-
-        sums = []
-        for t in range(PACK):
-            for i in range(2):
-                nc.vector.tensor_tensor(g[t][:, i, :], d_tr[t, i], damp[t, i], ALU.mult)
-            if t < last:
-                total = psum.tile([P, V], F32, name="total", tag="bank%d" % (5 + t))
-                for a in range(2):
-                    for i in range(2):
-                        back(total[:, a * P : (a + 1) * P], t, i, a)
-                sums.append(total)
-            else:
-                last_sums = [psum.tile([P, P], F32, name="total", tag=tag) for tag in ("bank4", "bank0")]
-                for i in range(2):
-                    for a in range(2):
-                        back(last_sums[a][:], t, i, a)
-            if t > 0:
-                step(t - 1, slice(0, V), sums[t - 1][:])
-                nc.sync.dma_start(out_rows[:, t - 1, :], y[:, t - 1, :])
-        for a in range(2):
-            step(last, slice(a * P, (a + 1) * P), last_sums[a][:])
-        nc.sync.dma_start(out_rows[:, last, :], y[:, last, :])
+        whole = slice(0, V)
+        for t in pairs[0]:
+            pull(t, whole)
+        for t in pairs[0]:
+            nc.vector.tensor_tensor(part[:, t, :], g[:, t, 0, :], hc[:, t, :], ALU.add)
+        for t in pairs[0]:
+            nc.vector.tensor_tensor(y[:, t, :], g[:, t, 1, :], part[:, t, :], ALU.add)
+        nc.sync.dma_start(out_rows[:, 0:2, :], y[:, 0:2, :])
 
         y_bf = sb.tile([P, V, PACK], BF16, name="y_bf", align_bytes=64)
         ysrc = y[:].rearrange("p t (c i) -> p c t i", i=4)
         ydst = y_bf[:].rearrange("p (c i) t -> p c t i", i=4)
         nc.scalar.copy(ydst[:, :, 0:2, :], ysrc[:, :, 0:2, :])
+
+        sides = [slice(0, P), slice(P, V)]
+        pull(2, whole)
+        for cols in sides:
+            pull(3, cols)
+        for cols in sides:
+            nc.vector.tensor_tensor(part[:, 2:4, cols], g[:, 2:4, 0, cols], hc[:, 2:4, cols], ALU.add)
+        for cols in sides:
+            nc.vector.tensor_tensor(y[:, 2:4, cols], g[:, 2:4, 1, cols], part[:, 2:4, cols], ALU.add)
+        nc.sync.dma_start(out_rows[:, 2:4, :], y[:, 2:4, :])
         for a in range(2):
             nc.vector.tensor_copy(ydst[:, 32 * a : 32 * (a + 1), 2:4, :], ysrc[:, 32 * a : 32 * (a + 1), 2:4, :])
         y_codes = sb.tile([P, V], U32, name="y_codes", align_bytes=64)

@@ -31,52 +31,62 @@ def tile_picked_ypm_pm_po_kernel(tc, x_words, x_scales, w1, rate, offs, cen, pos
         cen_t = lists.tile([P, V // 16], U16, name="cen_t")
         pos_t = [lists.tile([P, V // 16], U16, name="pos%d" % i) for i in range(2)]
 
-        xs_all = sb.tile([P, T], U8, name="xs_all", align_bytes=64)
-        xw_all = sb.tile([P, T], I32, name="xw_all", align_bytes=64)
+        xs_all = sb.tile([P, T], U8, name="xs_all", tag="scales_then_codes", align_bytes=64)
         w_raw = sb.tile([P, PACK, N], F32, name="w_raw", align_bytes=64)
         rate_t = sb.tile([P, PACK], F32, name="rate_t")
-        warm = sb.tile([P, 8], F32, name="warm")
+        warm = sb.tile([P, 8], F32, name="warm", tag="warm_then_words", align_bytes=64)
         warm2 = sb.tile([P, 8], F32, name="warm2")
 
-        nc.vector.memset(xs_all[:].bitcast(I32), 0)
-        nc.gpsimd.memset(warm[:], 1.0)
+        nc.gpsimd.memset(xs_all[:].bitcast(I32), 0)
+        nc.vector.memset(warm[:], 1.0)
         nc.scalar.activation(warm2[:], warm[:], ACT.Abs_reciprocal_sqrt)
+        xw_all = sb.tile([P, T], I32, name="xw_all", tag="warm_then_words", align_bytes=64)
 
-        nc.sync.dma_start(w_raw[:], w1.rearrange("(p j) n -> p j n", j=PACK))
-        for q in range(4):
-            nc.sync.dma_start(xs_all[32 * q : 32 * q + 4, :].bitcast(I32), x_scales[0, 4 * q : 4 * q + 4, :].bitcast(I32))
         nc.sync.dma_start(offs_t[:], offs)
-        nc.sync.dma_start(xw_all[:], x_words[0].rearrange("p c r -> p (c r)").bitcast(I32))
         nc.sync.dma_start(cen_t[:], cen)
+        nc.sync.dma_start(w_raw[:], w1.rearrange("(p j) n -> p j n", j=PACK))
         nc.sync.dma_start(pos_t[0][:], pos1)
         nc.sync.dma_start(pos_t[1][:], pos2)
-        nc.sync.dma_start(rate_t[:], rate.rearrange("(p t) o -> p (t o)", t=PACK))
+        for q in range(4):
+            nc.sync.dma_start(xs_all[32 * q : 32 * q + 4, :].bitcast(I32), x_scales[0, 4 * q : 4 * q + 4, :].bitcast(I32))
+        nc.sync.dma_start(xw_all[:], x_words[0].rearrange("p c r -> p (c r)").bitcast(I32))
+        nc.gpsimd.dma_start(rate_t[:], rate.rearrange("(p t) o -> p (t o)", t=PACK))
 
         xs = sb.tile([P, S], U8, name="xs", align_bytes=64)
         nc.vector.tensor_copy(xs[:], xs_all[:].indirect(offs_t[:]))
 
-        w_bf = sb.tile([P, PACK, P, PACK], BF16, name="w_bf", align_bytes=64)
+        w_bf = [sb.tile([P, 2, P, PACK], BF16, name="w_bf%d" % u, align_bytes=64) for u in range(2)]
         src = w_raw[:].rearrange("p j (m t) -> p m j t", t=PACK)
-        dst = w_bf[:].rearrange("p t m j -> p m j t")
-        nc.scalar.copy(dst[:, 0:64], src[:, 0:64])
-        nc.vector.tensor_copy(dst[:, 64:P], src[:, 64:P])
-        w_codes = sb.tile([P, N], U32, name="w_codes", align_bytes=64)
-        w_scales = sb.tile([P, N], U8, name="w_scales", align_bytes=64)
-        nc.vector.quantize_mx(out=w_codes[:].bitcast(FP8X4), scales=w_scales[:], in_=w_bf[:].rearrange("p t m j -> p (t m j)"))
+        dst = [w_bf[u][:].rearrange("p t m j -> p m j t") for u in range(2)]
+        nc.scalar.copy(dst[0][:, 0:96], src[:, 0:96, :, 0:2])
+        nc.vector.tensor_copy(dst[0][:, 96:P], src[:, 96:P, :, 0:2])
+        nc.scalar.copy(dst[1], src[:, :, :, 2:4])
+        w_codes, w_scales = [], []
 
+        def quantise_weights(u, tag):
+            w_codes.append(sb.tile([P, 2 * P], U32, name="w_codes", tag=tag, align_bytes=64))
+            w_scales.append(sb.tile([P, 2 * P], U8, name="w_scales%d" % u, align_bytes=64))
+            nc.vector.quantize_mx(
+                out=w_codes[u][:].bitcast(FP8X4),
+                scales=w_scales[u][:],
+                in_=w_bf[u][:].rearrange("p t m j -> p (t m j)"),
+            )
+
+        quantise_weights(0, "scales_then_codes")
         xw = sb.tile([P, S], U32, name="xw", align_bytes=64)
         for a in range(2):
             nc.vector.tensor_copy(
                 xw[:, a * HALF : (a + 1) * HALF],
                 xw_all[:].bitcast(U32).indirect(offs_t[:, a * HALF // 16 : (a + 1) * HALF // 16]),
             )
+        quantise_weights(1, "warm_then_words")
 
         def product(t, cols, name):
             acc = psum.tile([P, cols.stop - cols.start], F32, name=name)
             nc.tensor.matmul_mx(
                 out=acc[:],
-                lhsT=w_codes[:, t * P : (t + 1) * P].bitcast(FP8X4),
-                lhsT_scale=w_scales[:, t * P : (t + 1) * P],
+                lhsT=w_codes[t // 2][:, t % 2 * P : (t % 2 + 1) * P].bitcast(FP8X4),
+                lhsT_scale=w_scales[t // 2][:, t % 2 * P : (t % 2 + 1) * P],
                 rhs=xw[:, cols].bitcast(FP8X4),
                 rhs_scale=xs[:, cols],
                 start=True,

@@ -17,50 +17,57 @@ ALU = mybir.AluOpType
 
 P = 128
 PACK = 4
+QUADRANTS = 4
+LIST_ROWS = 16
 HALF = S // 2
+SCALAR_CAST_COLUMNS = 96
 
 
-def tile_picked_ypm_pm_po_kernel(tc, x_words, x_scales, w1, rate, offs, cen, pos1, pos2, out_0, out_1, out_2):
+def tile_picked_ypm_pm_po_kernel(
+    tc, x_words, x_scales, w1, rate, offs, cen, pos1, pos2, out_0, out_1, out_2
+):
     nc = tc.nc
     with ExitStack() as ctx:
         lists = ctx.enter_context(tc.tile_pool(name="lists", bufs=1))
         sb = ctx.enter_context(tc.tile_pool(name="sb", bufs=1))
         psum = ctx.enter_context(tc.psum_pool(name="psum", bufs=1))
 
-        offs_t = lists.tile([P, S // 16], U16, name="offs_t")
-        cen_t = lists.tile([P, V // 16], U16, name="cen_t")
-        pos_t = [lists.tile([P, V // 16], U16, name="pos%d" % i) for i in range(2)]
+        offs_t = lists.tile([P, S // LIST_ROWS], U16, name="offs_t")
+        cen_t = lists.tile([P, V // LIST_ROWS], U16, name="cen_t")
+        pos_t = [lists.tile([P, V // LIST_ROWS], U16, name="pos%d" % i) for i in range(2)]
 
-        xs_all = sb.tile([P, T], U8, name="xs_all", tag="scales_then_codes", align_bytes=64)
+        x_scales_all = sb.tile([P, T], U8, name="x_scales_all", tag="scales_then_codes", align_bytes=64)
+        x_words_all = sb.tile([P, T], I32, name="x_words_all", tag="words_then_codes", align_bytes=64)
         w_raw = sb.tile([P, PACK, N], F32, name="w_raw", align_bytes=64)
         rate_t = sb.tile([P, PACK], F32, name="rate_t")
-        warm = sb.tile([P, 8], F32, name="warm", tag="warm_then_words", align_bytes=64)
-        warm2 = sb.tile([P, 8], F32, name="warm2")
+        one_in = sb.tile([P, 1], F32, name="one_in")
+        one = sb.tile([P, 1], F32, name="one")
 
-        nc.gpsimd.memset(xs_all[:].bitcast(I32), 0)
-        nc.vector.memset(warm[:], 1.0)
-        nc.scalar.activation(warm2[:], warm[:], ACT.Abs_reciprocal_sqrt)
-        xw_all = sb.tile([P, T], I32, name="xw_all", tag="warm_then_words", align_bytes=64)
+        nc.gpsimd.memset(x_scales_all[:].bitcast(I32), 0)
+        nc.vector.memset(one_in[:], 1.0)
+        nc.scalar.activation(one[:], one_in[:], ACT.Abs_reciprocal_sqrt)
 
-        nc.sync.dma_start(offs_t[:], offs)
-        nc.sync.dma_start(cen_t[:], cen)
         nc.sync.dma_start(w_raw[:], w1.rearrange("(p j) n -> p j n", j=PACK))
+        for q in range(QUADRANTS):
+            nc.sync.dma_start(
+                x_scales_all[32 * q : 32 * q + 4, :].bitcast(I32), x_scales[0, 4 * q : 4 * q + 4, :].bitcast(I32)
+            )
+        nc.sync.dma_start(offs_t[:], offs)
+        nc.sync.dma_start(x_words_all[:], x_words[0].rearrange("p c r -> p (c r)").bitcast(I32))
+        nc.sync.dma_start(cen_t[:], cen)
         nc.sync.dma_start(pos_t[0][:], pos1)
         nc.sync.dma_start(pos_t[1][:], pos2)
-        for q in range(4):
-            nc.sync.dma_start(xs_all[32 * q : 32 * q + 4, :].bitcast(I32), x_scales[0, 4 * q : 4 * q + 4, :].bitcast(I32))
-        nc.sync.dma_start(xw_all[:], x_words[0].rearrange("p c r -> p (c r)").bitcast(I32))
-        nc.gpsimd.dma_start(rate_t[:], rate.rearrange("(p t) o -> p (t o)", t=PACK))
+        nc.sync.dma_start(rate_t[:], rate.rearrange("(p t) o -> p (t o)", t=PACK))
 
-        xs = sb.tile([P, S], U8, name="xs", align_bytes=64)
-        nc.vector.tensor_copy(xs[:], xs_all[:].indirect(offs_t[:]))
+        x_scales_picked = sb.tile([P, S], U8, name="x_scales_picked", align_bytes=64)
+        nc.vector.tensor_copy(x_scales_picked[:], x_scales_all[:].indirect(offs_t[:]))
 
         w_bf = [sb.tile([P, 2, P, PACK], BF16, name="w_bf%d" % u, align_bytes=64) for u in range(2)]
-        src = w_raw[:].rearrange("p j (m t) -> p m j t", t=PACK)
-        dst = [w_bf[u][:].rearrange("p t m j -> p m j t") for u in range(2)]
-        nc.scalar.copy(dst[0][:, 0:96], src[:, 0:96, :, 0:2])
-        nc.vector.tensor_copy(dst[0][:, 96:P], src[:, 96:P, :, 0:2])
-        nc.scalar.copy(dst[1], src[:, :, :, 2:4])
+        w_src = w_raw[:].rearrange("p j (m t) -> p m j t", t=PACK)
+        w_dst = [w_bf[u][:].rearrange("p s m j -> p m j s") for u in range(2)]
+        nc.scalar.copy(w_dst[0][:, 0:SCALAR_CAST_COLUMNS], w_src[:, 0:SCALAR_CAST_COLUMNS, :, 0:2])
+        nc.vector.tensor_copy(w_dst[0][:, SCALAR_CAST_COLUMNS:P], w_src[:, SCALAR_CAST_COLUMNS:P, :, 0:2])
+        nc.scalar.copy(w_dst[1], w_src[:, :, :, 2:4])
         w_codes, w_scales = [], []
 
         def quantise_weights(u, tag):
@@ -69,49 +76,50 @@ def tile_picked_ypm_pm_po_kernel(tc, x_words, x_scales, w1, rate, offs, cen, pos
             nc.vector.quantize_mx(
                 out=w_codes[u][:].bitcast(FP8X4),
                 scales=w_scales[u][:],
-                in_=w_bf[u][:].rearrange("p t m j -> p (t m j)"),
+                in_=w_bf[u][:].rearrange("p s m j -> p (s m j)"),
             )
 
         quantise_weights(0, "scales_then_codes")
-        xw = sb.tile([P, S], U32, name="xw", align_bytes=64)
+        x_words_picked = sb.tile([P, S], U32, name="x_words_picked", align_bytes=64)
         for a in range(2):
             nc.vector.tensor_copy(
-                xw[:, a * HALF : (a + 1) * HALF],
-                xw_all[:].bitcast(U32).indirect(offs_t[:, a * HALF // 16 : (a + 1) * HALF // 16]),
+                x_words_picked[:, a * HALF : (a + 1) * HALF],
+                x_words_all[:].bitcast(U32).indirect(offs_t[:, a * HALF // LIST_ROWS : (a + 1) * HALF // LIST_ROWS]),
             )
-        quantise_weights(1, "warm_then_words")
+        quantise_weights(1, "words_then_codes")
 
         def product(t, cols, name):
             acc = psum.tile([P, cols.stop - cols.start], F32, name=name)
+            tile_cols = slice(t % 2 * P, (t % 2 + 1) * P)
             nc.tensor.matmul_mx(
                 out=acc[:],
-                lhsT=w_codes[t // 2][:, t % 2 * P : (t % 2 + 1) * P].bitcast(FP8X4),
-                lhsT_scale=w_scales[t // 2][:, t % 2 * P : (t % 2 + 1) * P],
-                rhs=xw[:, cols].bitcast(FP8X4),
-                rhs_scale=xs[:, cols],
+                lhsT=w_codes[t // 2][:, tile_cols].bitcast(FP8X4),
+                lhsT_scale=w_scales[t // 2][:, tile_cols],
+                rhs=x_words_picked[:, cols].bitcast(FP8X4),
+                rhs_scale=x_scales_picked[:, cols],
                 start=True,
                 stop=True,
             )
             return acc
 
         h = [sb.tile([P, S], F32, name="h%d" % t) for t in range(PACK)]
-        halves = [slice(0, HALF), slice(HALF, S)]
-        for a, cols in enumerate(halves):
-            for t in range(2):
+        vertex_halves = [slice(0, HALF), slice(HALF, S)]
+        pairs = [(0, 1), (2, 3)]
+        for a, cols in enumerate(vertex_halves):
+            for t in pairs[0]:
                 nc.scalar.copy(h[t][:, cols], product(t, cols, "acc%d_%d" % (t, a))[:])
-        accs = {t: product(t, slice(0, S), "acc%d" % t) for t in range(2, PACK)}
-        for cols in halves:
-            for t in range(2, PACK):
+        accs = {t: product(t, slice(0, S), "acc%d" % t) for t in pairs[1]}
+        for cols in vertex_halves:
+            for t in pairs[1]:
                 nc.scalar.copy(h[t][:, cols], accs[t][:, cols])
 
         hc = sb.tile([P, PACK, V], F32, name="hc")
         y = sb.tile([P, PACK, V], F32, name="y")
         d = [sb.tile([P, 2, V], F32, name="d%d" % t) for t in range(PACK)]
-        work = [sb.tile([P, 2, V], F32, name="work%d" % u) for u in range(2)]
+        work = [sb.tile([P, 2, V], F32, name="work%d" % s) for s in range(2)]
         damp = [sb.tile([P, 2, V], F32, name="damp%d" % t) for t in range(PACK)]
         g = sb.tile([P, PACK, 2, V], F32, name="g")
         part = sb.tile([P, PACK, V], F32, name="part")
-        pairs = [(0, 1), (2, 3)]
         for pair in pairs:
             for t in pair:
                 nc.vector.tensor_copy(hc[:, t, :], h[t][:].indirect(cen_t[:]))
@@ -122,18 +130,20 @@ def tile_picked_ypm_pm_po_kernel(tc, x_words, x_scales, w1, rate, offs, cen, pos
                 for i in range(2):
                     nc.scalar.activation(work[t % 2][:, i, :], d[t][:, i, :], ACT.Square)
             for t in pair:
-                nc.scalar.activation(work[t % 2][:], work[t % 2][:], ACT.Abs_reciprocal_sqrt, bias=1.0)
+                nc.scalar.activation(work[t % 2][:], work[t % 2][:], ACT.Abs_reciprocal_sqrt, bias=one[:])
             for t in pair:
                 nc.scalar.activation(damp[t][:], work[t % 2][:], ACT.Square)
 
         out_rows = out_0.rearrange("(p t) v -> p t v", t=PACK)
 
         def pull(t, cols):
-            nc.vector.scalar_tensor_tensor(g[:, t, :, cols], d[t][:, :, cols], rate_t[:, t : t + 1], damp[t][:, :, cols], ALU.mult, ALU.mult)
+            nc.vector.scalar_tensor_tensor(
+                g[:, t, :, cols], d[t][:, :, cols], rate_t[:, t : t + 1], damp[t][:, :, cols], ALU.mult, ALU.mult
+            )
 
-        whole = slice(0, V)
+        all_centres = slice(0, V)
         for t in pairs[0]:
-            pull(t, whole)
+            pull(t, all_centres)
         for t in pairs[0]:
             nc.vector.tensor_tensor(part[:, t, :], g[:, t, 0, :], hc[:, t, :], ALU.add)
         for t in pairs[0]:
@@ -141,27 +151,34 @@ def tile_picked_ypm_pm_po_kernel(tc, x_words, x_scales, w1, rate, offs, cen, pos
         nc.sync.dma_start(out_rows[:, 0:2, :], y[:, 0:2, :])
 
         y_bf = sb.tile([P, V, PACK], BF16, name="y_bf", align_bytes=64)
-        ysrc = y[:].rearrange("p t (c i) -> p c t i", i=4)
-        ydst = y_bf[:].rearrange("p (c i) t -> p c t i", i=4)
-        nc.scalar.copy(ydst[:, :, 0:2, :], ysrc[:, :, 0:2, :])
+        run = 4
+        y_src = y[:].rearrange("p t (c r) -> p c t r", r=run)
+        y_dst = y_bf[:].rearrange("p (c r) t -> p c t r", r=run)
+        nc.scalar.copy(y_dst[:, :, 0:2, :], y_src[:, :, 0:2, :])
 
-        sides = [slice(0, P), slice(P, V)]
-        pull(2, whole)
-        for cols in sides:
+        centre_halves = [slice(0, V // 2), slice(V // 2, V)]
+        pull(2, all_centres)
+        for cols in centre_halves:
             pull(3, cols)
-        for cols in sides:
+        for cols in centre_halves:
             nc.vector.tensor_tensor(part[:, 2:4, cols], g[:, 2:4, 0, cols], hc[:, 2:4, cols], ALU.add)
-        for cols in sides:
+        for cols in centre_halves:
             nc.vector.tensor_tensor(y[:, 2:4, cols], g[:, 2:4, 1, cols], part[:, 2:4, cols], ALU.add)
         nc.sync.dma_start(out_rows[:, 2:4, :], y[:, 2:4, :])
-        for a in range(2):
-            nc.vector.tensor_copy(ydst[:, 32 * a : 32 * (a + 1), 2:4, :], ysrc[:, 32 * a : 32 * (a + 1), 2:4, :])
+        for cols in centre_halves:
+            runs = slice(cols.start // run, cols.stop // run)
+            nc.vector.tensor_copy(y_dst[:, runs, 2:4, :], y_src[:, runs, 2:4, :])
         y_codes = sb.tile([P, V], U32, name="y_codes", align_bytes=64)
         y_scales = sb.tile([P, V], U8, name="y_scales", align_bytes=64)
-        for a in range(2):
-            cols = slice(a * P, (a + 1) * P)
-            nc.vector.quantize_mx(out=y_codes[:, cols].bitcast(FP8X4), scales=y_scales[:, cols], in_=y_bf[:, cols, :].rearrange("p v t -> p (v t)"))
+        for cols in centre_halves:
+            nc.vector.quantize_mx(
+                out=y_codes[:, cols].bitcast(FP8X4),
+                scales=y_scales[:, cols],
+                in_=y_bf[:, cols, :].rearrange("p v t -> p (v t)"),
+            )
         nc.scalar.dma_start(out_1[0].rearrange("p c r -> p (c r)").bitcast(I32), y_codes[:].bitcast(I32))
-        for q in range(4):
-            eng = nc.scalar if q == 3 else nc.sync
-            eng.dma_start(out_2[0, 4 * q : 4 * q + 4, :].bitcast(I32), y_scales[32 * q : 32 * q + 4, :].bitcast(I32))
+        for q in range(QUADRANTS):
+            queue = nc.scalar if q == QUADRANTS - 1 else nc.sync
+            queue.dma_start(
+                out_2[0, 4 * q : 4 * q + 4, :].bitcast(I32), y_scales[32 * q : 32 * q + 4, :].bitcast(I32)
+            )

@@ -48,10 +48,8 @@ def tile_picked_ypm_pm_po_kernel(
         nc.scalar.activation(one[:], one_in[:], ACT.Abs_reciprocal_sqrt)
 
         nc.sync.dma_start(w_raw[:], w1.rearrange("(p j) n -> p j n", j=PACK))
-        for q in range(QUADRANTS):
-            nc.sync.dma_start(
-                x_scales_all[32 * q : 32 * q + 4, :].bitcast(I32), x_scales[0, 4 * q : 4 * q + 4, :].bitcast(I32)
-            )
+        for r in range(4):
+            nc.sync.dma_start(x_scales_all[r:P:32, :].bitcast(I32), x_scales[0, r:16:4, :].bitcast(I32))
         nc.sync.dma_start(offs_t[:], offs)
         nc.sync.dma_start(x_words_all[:], x_words[0].rearrange("p c r -> p (c r)").bitcast(I32))
         nc.sync.dma_start(cen_t[:], cen)
@@ -176,9 +174,7 @@ def tile_picked_ypm_pm_po_kernel(
                 scales=y_scales[:, cols],
                 in_=y_bf[:, cols, :].rearrange("p v t -> p (v t)"),
             )
-        nc.scalar.dma_start(out_1[0].rearrange("p c r -> p (c r)").bitcast(I32), y_codes[:].bitcast(I32))
-        for q in range(QUADRANTS):
-            queue = nc.scalar if q == QUADRANTS - 1 else nc.sync
-            queue.dma_start(
-                out_2[0, 4 * q : 4 * q + 4, :].bitcast(I32), y_scales[32 * q : 32 * q + 4, :].bitcast(I32)
-            )
+        nc.sync.dma_start(out_1[0].rearrange("p c r -> p (c r)").bitcast(I32), y_codes[:].bitcast(I32))
+        for r in range(4):
+            queue = nc.scalar if r < 3 else nc.sync
+            queue.dma_start(out_2[0, r:16:4, :].bitcast(I32), y_scales[r:P:32, :].bitcast(I32))

@@ -38,27 +38,30 @@ def tile_picked_ypm_pm_po_kernel(
 
         x_scales_all = sb.tile([P, T], U8, name="x_scales_all", tag="scales_then_codes", align_bytes=64)
         x_words_all = sb.tile([P, T], I32, name="x_words_all", tag="words_then_codes", align_bytes=64)
-        w_raw = sb.tile([P, PACK, N], F32, name="w_raw", align_bytes=64)
-        rate_t = sb.tile([P, PACK], F32, name="rate_t")
+        w_raw = sb.tile([P, PACK, N], F32, name="w_raw", tag="raw_then_rate", align_bytes=64)
         one_in = sb.tile([P, 1], F32, name="one_in")
         one = sb.tile([P, 1], F32, name="one")
 
-        nc.gpsimd.memset(x_scales_all[:].bitcast(I32), 0)
+        nc.scalar.dma_start(x_scales_all[16:32, :].bitcast(I32), x_scales[0].bitcast(I32))
+        nc.gpsimd.memset(x_scales_all[0:16, :].bitcast(I32), 0)
+        for rows in (slice(32, 64), slice(64, P)):
+            nc.vector.memset(x_scales_all[rows, :].bitcast(I32), 0)
+        x_scales_placed = sb.tile([P, S], U8, name="x_scales_placed", align_bytes=64)
+        nc.gpsimd.memset(x_scales_placed[:].bitcast(I32), 0)
         nc.vector.memset(one_in[:], 1.0)
         nc.scalar.activation(one[:], one_in[:], ACT.Abs_reciprocal_sqrt)
 
-        nc.sync.dma_start(w_raw[:], w1.rearrange("(p j) n -> p j n", j=PACK))
-        for r in range(4):
-            nc.sync.dma_start(x_scales_all[r:P:32, :].bitcast(I32), x_scales[0, r:16:4, :].bitcast(I32))
         nc.sync.dma_start(offs_t[:], offs)
+        nc.sync.dma_start(w_raw[:], w1.rearrange("(p j) n -> p j n", j=PACK))
         nc.sync.dma_start(x_words_all[:], x_words[0].rearrange("p c r -> p (c r)").bitcast(I32))
         nc.sync.dma_start(cen_t[:], cen)
         nc.sync.dma_start(pos_t[0][:], pos1)
         nc.sync.dma_start(pos_t[1][:], pos2)
-        nc.sync.dma_start(rate_t[:], rate.rearrange("(p t) o -> p (t o)", t=PACK))
 
         x_scales_picked = sb.tile([P, S], U8, name="x_scales_picked", align_bytes=64)
         nc.vector.tensor_copy(x_scales_picked[:], x_scales_all[:].indirect(offs_t[:]))
+        for r in range(4):
+            nc.scalar.dma_start(x_scales_placed[r:P:32, :].bitcast(I32), x_scales_picked[16 + r : 32 : 4, :].bitcast(I32))
 
         w_bf = [sb.tile([P, 2, P, PACK], BF16, name="w_bf%d" % u, align_bytes=64) for u in range(2)]
         w_src = w_raw[:].rearrange("p j (m t) -> p m j t", t=PACK)
@@ -66,6 +69,8 @@ def tile_picked_ypm_pm_po_kernel(
         nc.scalar.copy(w_dst[0][:, 0:SCALAR_CAST_COLUMNS], w_src[:, 0:SCALAR_CAST_COLUMNS, :, 0:2])
         nc.vector.tensor_copy(w_dst[0][:, SCALAR_CAST_COLUMNS:P], w_src[:, SCALAR_CAST_COLUMNS:P, :, 0:2])
         nc.scalar.copy(w_dst[1], w_src[:, :, :, 2:4])
+        rate_t = sb.tile([P, PACK], F32, name="rate_t", tag="raw_then_rate", align_bytes=64)
+        nc.sync.dma_start(rate_t[:], rate.rearrange("(p t) o -> p (t o)", t=PACK))
         w_codes, w_scales = [], []
 
         def quantise_weights(u, tag):
@@ -94,7 +99,7 @@ def tile_picked_ypm_pm_po_kernel(
                 lhsT=w_codes[t // 2][:, tile_cols].bitcast(FP8X4),
                 lhsT_scale=w_scales[t // 2][:, tile_cols],
                 rhs=x_words_picked[:, cols].bitcast(FP8X4),
-                rhs_scale=x_scales_picked[:, cols],
+                rhs_scale=x_scales_placed[:, cols],
                 start=True,
                 stop=True,
             )

@@ -51,8 +51,10 @@ def tile_picked_ypm_pm_po_kernel(
         nc.vector.memset(one_in[:], 1.0)
         nc.scalar.activation(one[:], one_in[:], ACT.Abs_reciprocal_sqrt)
 
+        w_rows = w1.rearrange("(p j) n -> p j n", j=PACK)
+        nc.sync.dma_start(w_raw[:, 0:1, :], w_rows[:, 0:1, :])
         nc.sync.dma_start(offs_t[:], offs)
-        nc.sync.dma_start(w_raw[:], w1.rearrange("(p j) n -> p j n", j=PACK))
+        nc.sync.dma_start(w_raw[:, 1:PACK, :], w_rows[:, 1:PACK, :])
         nc.sync.dma_start(x_words_all[:], x_words[0].rearrange("p c r -> p (c r)").bitcast(I32))
         nc.sync.dma_start(cen_t[:], cen)
         nc.sync.dma_start(pos_t[0][:], pos1)
@@ -75,7 +77,7 @@ def tile_picked_ypm_pm_po_kernel(
 
         def quantise_weights(u, tag):
             w_codes.append(sb.tile([P, 2 * P], U32, name="w_codes", tag=tag, align_bytes=64))
-            w_scales.append(sb.tile([P, 2 * P], U8, name="w_scales%d" % u, align_bytes=64))
+            w_scales.append(sb.tile([P, 2 * P], U8, name="w_scales", tag="w_scales%d" % u, align_bytes=64))
             nc.vector.quantize_mx(
                 out=w_codes[u][:].bitcast(FP8X4),
                 scales=w_scales[u][:],
@@ -108,69 +110,97 @@ def tile_picked_ypm_pm_po_kernel(
         h = [sb.tile([P, S], F32, name="h%d" % t) for t in range(PACK)]
         vertex_halves = [slice(0, HALF), slice(HALF, S)]
         pairs = [(0, 1), (2, 3)]
-        for a, cols in enumerate(vertex_halves):
-            for t in pairs[0]:
-                nc.scalar.copy(h[t][:, cols], product(t, cols, "acc%d_%d" % (t, a))[:])
+        for t in pairs[0]:
+            nc.scalar.copy(h[t][:, vertex_halves[0]], product(t, vertex_halves[0], "acc%d_0" % t)[:])
+        third, fourth = slice(HALF, HALF + P), slice(HALF + P, S)
+        nc.scalar.copy(h[0][:, third], product(0, third, "acc0_1")[:])
+        nc.vector.tensor_copy(h[0][:, fourth], product(0, fourth, "acc0_2")[:])
+        nc.scalar.copy(h[1][:, vertex_halves[1]], product(1, vertex_halves[1], "acc1_1")[:])
         accs = {t: product(t, slice(0, S), "acc%d" % t) for t in pairs[1]}
         for cols in vertex_halves:
             for t in pairs[1]:
                 nc.scalar.copy(h[t][:, cols], accs[t][:, cols])
 
         hc = sb.tile([P, PACK, V], F32, name="hc")
-        y = sb.tile([P, PACK, V], F32, name="y")
         d = [sb.tile([P, 2, V], F32, name="d%d" % t) for t in range(PACK)]
-        work = [sb.tile([P, 2, V], F32, name="work%d" % s) for s in range(2)]
         damp = [sb.tile([P, 2, V], F32, name="damp%d" % t) for t in range(PACK)]
         g = sb.tile([P, PACK, 2, V], F32, name="g")
-        part = sb.tile([P, PACK, V], F32, name="part")
         for pair in pairs:
             for t in pair:
                 nc.vector.tensor_copy(hc[:, t, :], h[t][:].indirect(cen_t[:]))
             for t in pair:
                 for i in range(2):
                     nc.vector.tensor_tensor(d[t][:, i, :], h[t][:].indirect(pos_t[i][:]), hc[:, t, :], ALU.subtract)
-            for t in pair:
-                for i in range(2):
-                    nc.scalar.activation(work[t % 2][:, i, :], d[t][:, i, :], ACT.Square)
-            for t in pair:
-                nc.scalar.activation(work[t % 2][:], work[t % 2][:], ACT.Abs_reciprocal_sqrt, bias=one[:])
-            for t in pair:
-                nc.scalar.activation(damp[t][:], work[t % 2][:], ACT.Square)
+
+        def work_tile(tag, columns):
+            return sb.tile([P, columns], F32, name="work", tag=tag, align_bytes=64)
+
+        def square(out, t, i):
+            nc.scalar.activation(out, d[t][:, i, :], ACT.Square)
+
+        def root(work):
+            nc.scalar.activation(work, work, ACT.Abs_reciprocal_sqrt, bias=one[:])
+
+        def damping(out, work):
+            nc.scalar.activation(out, work, ACT.Square)
+
+        flat = "p i v -> p (i v)"
+        work0, wide = work_tile("words_then_codes", 2 * V), work_tile("w_scales1", 3 * V)
+        work1, work30, work31 = wide[:, 0 : 2 * V], wide[:, 0:V], wide[:, V : 2 * V]
+        square(work0[:, 0:V], 0, 0)
+        square(work0[:, V : 2 * V], 0, 1)
+        square(work30, 1, 0)
+        root(work0[:])
+        square(work31, 1, 1)
+        damping(damp[0][:].rearrange(flat), work0[:])
+        root(work1)
+        square(work0[:, 0:V], 2, 0)
+        damping(damp[1][:].rearrange(flat), work1)
+        square(work0[:, V : 2 * V], 2, 1)
+        square(work30, 3, 0)
+        root(work0[:])
+        square(work31, 3, 1)
+        damping(damp[2][:].rearrange(flat), work0[:])
+        root(work30)
+        root(work31)
+        damping(damp[3][:, 0, :], work30)
+        damping(damp[3][:, 1, :], work31)
 
         out_rows = out_0.rearrange("(p t) v -> p t v", t=PACK)
 
-        def pull(t, cols):
+        def pull(t, i):
             nc.vector.scalar_tensor_tensor(
-                g[:, t, :, cols], d[t][:, :, cols], rate_t[:, t : t + 1], damp[t][:, :, cols], ALU.mult, ALU.mult
+                g[:, t, i, :], d[t][:, i, :], rate_t[:, t : t + 1], damp[t][:, i, :], ALU.mult, ALU.mult
             )
 
-        all_centres = slice(0, V)
-        for t in pairs[0]:
-            pull(t, all_centres)
-        for t in pairs[0]:
-            nc.vector.tensor_tensor(part[:, t, :], g[:, t, 0, :], hc[:, t, :], ALU.add)
-        for t in pairs[0]:
-            nc.vector.tensor_tensor(y[:, t, :], g[:, t, 1, :], part[:, t, :], ALU.add)
-        nc.sync.dma_start(out_rows[:, 0:2, :], y[:, 0:2, :])
-
+        centre_halves = [slice(0, V // 2), slice(V // 2, V)]
         y_bf = sb.tile([P, V, PACK], BF16, name="y_bf", align_bytes=64)
         run = 4
-        y_src = y[:].rearrange("p t (c r) -> p c t r", r=run)
         y_dst = y_bf[:].rearrange("p (c r) t -> p c t r", r=run)
-        nc.scalar.copy(y_dst[:, :, 0:2, :], y_src[:, :, 0:2, :])
-
-        centre_halves = [slice(0, V // 2), slice(V // 2, V)]
-        pull(2, all_centres)
+        pull(0, slice(0, 2))
+        for i in range(2):
+            pull(1, i)
+        part01 = sb.tile([P, 2, V], F32, name="part01")
+        nc.vector.tensor_tensor(part01[:], g[:, 0:2, 0, :], hc[:, 0:2, :], ALU.add)
+        pull(2, slice(0, 2))
+        y01 = sb.tile([P, 2, V], F32, name="y01", tag="words_then_codes", align_bytes=64)
+        nc.vector.tensor_tensor(y01[:], g[:, 0:2, 1, :], part01[:], ALU.add)
+        nc.sync.dma_start(out_rows[:, 0:2, :], y01[:])
+        nc.scalar.copy(y_dst[:, :, 0:2, :], y01[:].rearrange("p t (c r) -> p c t r", r=run))
+        for i in range(2):
+            pull(3, i)
+        part23 = wide[:, V : 3 * V].rearrange("p (t v) -> p t v", t=2)
+        y23 = sb.tile([P, 2, V], F32, name="y23")
         for cols in centre_halves:
-            pull(3, cols)
+            nc.vector.tensor_tensor(part23[:, :, cols], g[:, 2:4, 0, cols], hc[:, 2:4, cols], ALU.add)
         for cols in centre_halves:
-            nc.vector.tensor_tensor(part[:, 2:4, cols], g[:, 2:4, 0, cols], hc[:, 2:4, cols], ALU.add)
-        for cols in centre_halves:
-            nc.vector.tensor_tensor(y[:, 2:4, cols], g[:, 2:4, 1, cols], part[:, 2:4, cols], ALU.add)
-        nc.sync.dma_start(out_rows[:, 2:4, :], y[:, 2:4, :])
+            nc.vector.tensor_tensor(y23[:, :, cols], g[:, 2:4, 1, cols], part23[:, :, cols], ALU.add)
+        nc.sync.dma_start(out_rows[:, 2:4, :], y23[:])
+        y_src = y23[:].rearrange("p t (c r) -> p c t r", r=run)
         for cols in centre_halves:
             runs = slice(cols.start // run, cols.stop // run)
-            nc.vector.tensor_copy(y_dst[:, runs, 2:4, :], y_src[:, runs, 2:4, :])
+            nc.vector.tensor_copy(y_dst[:, runs, 2:4, :], y_src[:, runs])
+        out_words = out_1[0].rearrange("p c r -> p (c r)").bitcast(I32)
         y_codes = sb.tile([P, V], U32, name="y_codes", align_bytes=64)
         y_scales = sb.tile([P, V], U8, name="y_scales", align_bytes=64)
         for cols in centre_halves:
@@ -179,7 +209,7 @@ def tile_picked_ypm_pm_po_kernel(
                 scales=y_scales[:, cols],
                 in_=y_bf[:, cols, :].rearrange("p v t -> p (v t)"),
             )
-        nc.sync.dma_start(out_1[0].rearrange("p c r -> p (c r)").bitcast(I32), y_codes[:].bitcast(I32))
+            nc.sync.dma_start(out_words[:, cols], y_codes[:, cols].bitcast(I32))
         for r in range(4):
             queue = nc.scalar if r < 3 else nc.sync
             queue.dma_start(out_2[0, r:16:4, :].bitcast(I32), y_scales[r:P:32, :].bitcast(I32))

@@ -17,7 +17,9 @@ ALU = mybir.AluOpType
 
 P = 128
 PACK = 4
-QUADRANTS = 4
+QUADRANT = 32
+SCALE_ROWS = 16
+QUADRANT_ROWS = 4
 LIST_ROWS = 16
 HALF = S // 2
 SCALAR_CAST_COLUMNS = 96
@@ -42,9 +44,9 @@ def tile_picked_ypm_pm_po_kernel(
         one_in = sb.tile([P, 1], F32, name="one_in")
         one = sb.tile([P, 1], F32, name="one")
 
-        nc.scalar.dma_start(x_scales_all[16:32, :].bitcast(I32), x_scales[0].bitcast(I32))
-        nc.gpsimd.memset(x_scales_all[0:16, :].bitcast(I32), 0)
-        for rows in (slice(32, 64), slice(64, P)):
+        nc.scalar.dma_start(x_scales_all[SCALE_ROWS:QUADRANT, :].bitcast(I32), x_scales[0].bitcast(I32))
+        nc.gpsimd.memset(x_scales_all[0:SCALE_ROWS, :].bitcast(I32), 0)
+        for rows in (slice(QUADRANT, 2 * QUADRANT), slice(2 * QUADRANT, P)):
             nc.vector.memset(x_scales_all[rows, :].bitcast(I32), 0)
         x_scales_placed = sb.tile([P, S], U8, name="x_scales_placed", align_bytes=64)
         nc.gpsimd.memset(x_scales_placed[:].bitcast(I32), 0)
@@ -62,8 +64,11 @@ def tile_picked_ypm_pm_po_kernel(
 
         x_scales_picked = sb.tile([P, S], U8, name="x_scales_picked", align_bytes=64)
         nc.vector.tensor_copy(x_scales_picked[:], x_scales_all[:].indirect(offs_t[:]))
-        for r in range(4):
-            nc.scalar.dma_start(x_scales_placed[r:P:32, :].bitcast(I32), x_scales_picked[16 + r : 32 : 4, :].bitcast(I32))
+        for r in range(QUADRANT_ROWS):
+            nc.scalar.dma_start(
+                x_scales_placed[r:P:QUADRANT, :].bitcast(I32),
+                x_scales_picked[SCALE_ROWS + r : QUADRANT : QUADRANT_ROWS, :].bitcast(I32),
+            )
 
         w_bf = [sb.tile([P, 2, P, PACK], BF16, name="w_bf%d" % u, align_bytes=64) for u in range(2)]
         w_src = w_raw[:].rearrange("p j (m t) -> p m j t", t=PACK)
@@ -132,39 +137,40 @@ def tile_picked_ypm_pm_po_kernel(
                 for i in range(2):
                     nc.vector.tensor_tensor(d[t][:, i, :], h[t][:].indirect(pos_t[i][:]), hc[:, t, :], ALU.subtract)
 
-        def work_tile(tag, columns):
-            return sb.tile([P, columns], F32, name="work", tag=tag, align_bytes=64)
+        work_even_tile = sb.tile([P, 2 * V], F32, name="work", tag="words_then_codes", align_bytes=64)
+        odd_then_part = sb.tile([P, 3 * V], F32, name="work", tag="w_scales1", align_bytes=64)
+        work_even = work_even_tile[:].rearrange("p (i v) -> p i v", i=2)
+        work_odd = odd_then_part[:, 0 : 2 * V].rearrange("p (i v) -> p i v", i=2)
+        work = [work_even, work_odd]
+        both = slice(0, 2)
 
-        def square(out, t, i):
-            nc.scalar.activation(out, d[t][:, i, :], ACT.Square)
+        def square(t, i):
+            nc.scalar.activation(work[t % 2][:, i, :], d[t][:, i, :], ACT.Square)
 
-        def root(work):
-            nc.scalar.activation(work, work, ACT.Abs_reciprocal_sqrt, bias=one[:])
+        def root(t, i):
+            nc.scalar.activation(work[t % 2][:, i, :], work[t % 2][:, i, :], ACT.Abs_reciprocal_sqrt, bias=one[:])
 
-        def damping(out, work):
-            nc.scalar.activation(out, work, ACT.Square)
+        def damping(t, i):
+            nc.scalar.activation(damp[t][:, i, :], work[t % 2][:, i, :], ACT.Square)
 
-        flat = "p i v -> p (i v)"
-        work0, wide = work_tile("words_then_codes", 2 * V), work_tile("w_scales1", 3 * V)
-        work1, work30, work31 = wide[:, 0 : 2 * V], wide[:, 0:V], wide[:, V : 2 * V]
-        square(work0[:, 0:V], 0, 0)
-        square(work0[:, V : 2 * V], 0, 1)
-        square(work30, 1, 0)
-        root(work0[:])
-        square(work31, 1, 1)
-        damping(damp[0][:].rearrange(flat), work0[:])
-        root(work1)
-        square(work0[:, 0:V], 2, 0)
-        damping(damp[1][:].rearrange(flat), work1)
-        square(work0[:, V : 2 * V], 2, 1)
-        square(work30, 3, 0)
-        root(work0[:])
-        square(work31, 3, 1)
-        damping(damp[2][:].rearrange(flat), work0[:])
-        root(work30)
-        root(work31)
-        damping(damp[3][:, 0, :], work30)
-        damping(damp[3][:, 1, :], work31)
+        square(0, 0)
+        square(0, 1)
+        square(1, 0)
+        root(0, both)
+        square(1, 1)
+        damping(0, both)
+        root(1, both)
+        square(2, 0)
+        damping(1, both)
+        square(2, 1)
+        square(3, 0)
+        root(2, both)
+        square(3, 1)
+        damping(2, both)
+        for i in range(2):
+            root(3, i)
+        for i in range(2):
+            damping(3, i)
 
         out_rows = out_0.rearrange("(p t) v -> p t v", t=PACK)
 
@@ -177,19 +183,21 @@ def tile_picked_ypm_pm_po_kernel(
         y_bf = sb.tile([P, V, PACK], BF16, name="y_bf", align_bytes=64)
         run = 4
         y_dst = y_bf[:].rearrange("p (c r) t -> p c t r", r=run)
-        pull(0, slice(0, 2))
+
+        pull(0, both)
         for i in range(2):
             pull(1, i)
         part01 = sb.tile([P, 2, V], F32, name="part01")
         nc.vector.tensor_tensor(part01[:], g[:, 0:2, 0, :], hc[:, 0:2, :], ALU.add)
-        pull(2, slice(0, 2))
+        pull(2, both)
         y01 = sb.tile([P, 2, V], F32, name="y01", tag="words_then_codes", align_bytes=64)
         nc.vector.tensor_tensor(y01[:], g[:, 0:2, 1, :], part01[:], ALU.add)
         nc.sync.dma_start(out_rows[:, 0:2, :], y01[:])
         nc.scalar.copy(y_dst[:, :, 0:2, :], y01[:].rearrange("p t (c r) -> p c t r", r=run))
+
         for i in range(2):
             pull(3, i)
-        part23 = wide[:, V : 3 * V].rearrange("p (t v) -> p t v", t=2)
+        part23 = odd_then_part[:, V : 3 * V].rearrange("p (t v) -> p t v", t=2)
         y23 = sb.tile([P, 2, V], F32, name="y23")
         for cols in centre_halves:
             nc.vector.tensor_tensor(part23[:, :, cols], g[:, 2:4, 0, cols], hc[:, 2:4, cols], ALU.add)
@@ -210,6 +218,8 @@ def tile_picked_ypm_pm_po_kernel(
                 in_=y_bf[:, cols, :].rearrange("p v t -> p (v t)"),
             )
             nc.sync.dma_start(out_words[:, cols], y_codes[:, cols].bitcast(I32))
-        for r in range(4):
-            queue = nc.scalar if r < 3 else nc.sync
-            queue.dma_start(out_2[0, r:16:4, :].bitcast(I32), y_scales[r:P:32, :].bitcast(I32))
+        for r in range(QUADRANT_ROWS):
+            queue = nc.scalar if r < QUADRANT_ROWS // 2 else nc.sync
+            queue.dma_start(
+                out_2[0, r:SCALE_ROWS:QUADRANT_ROWS, :].bitcast(I32), y_scales[r:P:QUADRANT, :].bitcast(I32)
+            )

@@ -219,7 +219,7 @@ def tile_picked_ypm_pm_po_kernel(
             )
             nc.sync.dma_start(out_words[:, cols], y_codes[:, cols].bitcast(I32))
         for r in range(QUADRANT_ROWS):
-            queue = nc.scalar if r < QUADRANT_ROWS // 2 else nc.sync
+            queue = nc.scalar if r == 0 else nc.sync
             queue.dma_start(
                 out_2[0, r:SCALE_ROWS:QUADRANT_ROWS, :].bitcast(I32), y_scales[r:P:QUADRANT, :].bitcast(I32)
             )

@@ -137,9 +137,9 @@ def tile_picked_ypm_pm_po_kernel(
                 for i in range(2):
                     nc.vector.tensor_tensor(d[t][:, i, :], h[t][:].indirect(pos_t[i][:]), hc[:, t, :], ALU.subtract)
 
-        work_even_tile = sb.tile([P, 2 * V], F32, name="work", tag="words_then_codes", align_bytes=64)
+        even_then_y = sb.tile([P, PACK, V], F32, name="work", tag="words_then_codes", align_bytes=64)
         odd_then_part = sb.tile([P, 3 * V], F32, name="work", tag="w_scales1", align_bytes=64)
-        work_even = work_even_tile[:].rearrange("p (i v) -> p i v", i=2)
+        work_even = even_then_y[:, 0:2, :]
         work_odd = odd_then_part[:, 0 : 2 * V].rearrange("p (i v) -> p i v", i=2)
         work = [work_even, work_odd]
         both = slice(0, 2)
@@ -190,24 +190,23 @@ def tile_picked_ypm_pm_po_kernel(
         part01 = sb.tile([P, 2, V], F32, name="part01")
         nc.vector.tensor_tensor(part01[:], g[:, 0:2, 0, :], hc[:, 0:2, :], ALU.add)
         pull(2, both)
-        y01 = sb.tile([P, 2, V], F32, name="y01", tag="words_then_codes", align_bytes=64)
-        nc.vector.tensor_tensor(y01[:], g[:, 0:2, 1, :], part01[:], ALU.add)
-        nc.sync.dma_start(out_rows[:, 0:2, :], y01[:])
-        nc.scalar.copy(y_dst[:, :, 0:2, :], y01[:].rearrange("p t (c r) -> p c t r", r=run))
+        y = even_then_y
+        nc.vector.tensor_tensor(y[:, 0:2, :], g[:, 0:2, 1, :], part01[:], ALU.add)
+        nc.sync.dma_start(out_rows[:, 0:2, :], y[:, 0:2, :])
 
         for i in range(2):
             pull(3, i)
         part23 = odd_then_part[:, V : 3 * V].rearrange("p (t v) -> p t v", t=2)
-        y23 = sb.tile([P, 2, V], F32, name="y23")
         for cols in centre_halves:
             nc.vector.tensor_tensor(part23[:, :, cols], g[:, 2:4, 0, cols], hc[:, 2:4, cols], ALU.add)
         for cols in centre_halves:
-            nc.vector.tensor_tensor(y23[:, :, cols], g[:, 2:4, 1, cols], part23[:, :, cols], ALU.add)
-        nc.sync.dma_start(out_rows[:, 2:4, :], y23[:])
-        y_src = y23[:].rearrange("p t (c r) -> p c t r", r=run)
-        for cols in centre_halves:
-            runs = slice(cols.start // run, cols.stop // run)
-            nc.vector.tensor_copy(y_dst[:, runs, 2:4, :], y_src[:, runs])
+            nc.vector.tensor_tensor(y[:, 2:4, cols], g[:, 2:4, 1, cols], part23[:, :, cols], ALU.add)
+        nc.sync.dma_start(out_rows[:, 2:4, :], y[:, 2:4, :])
+        y_src = y[:].rearrange("p t (c r) -> p c t r", r=run)
+        quarter = V // 4 // run
+        nc.scalar.copy(y_dst[:, quarter : 2 * quarter], y_src[:, quarter : 2 * quarter])
+        nc.vector.tensor_copy(y_dst[:, 0:quarter], y_src[:, 0:quarter])
+        nc.vector.tensor_copy(y_dst[:, 2 * quarter :], y_src[:, 2 * quarter :])
         out_words = out_1[0].rearrange("p c r -> p (c r)").bitcast(I32)
         y_codes = sb.tile([P, V], U32, name="y_codes", align_bytes=64)
         y_scales = sb.tile([P, V], U8, name="y_scales", align_bytes=64)

@@ -118,8 +118,8 @@ def tile_picked_ypm_pm_po_kernel(
         for t in pairs[0]:
             nc.scalar.copy(h[t][:, vertex_halves[0]], product(t, vertex_halves[0], "acc%d_0" % t)[:])
         third, fourth = slice(HALF, HALF + P), slice(HALF + P, S)
-        nc.scalar.copy(h[0][:, third], product(0, third, "acc0_1")[:])
-        nc.vector.tensor_copy(h[0][:, fourth], product(0, fourth, "acc0_2")[:])
+        nc.vector.tensor_copy(h[0][:, third], product(0, third, "acc0_1")[:])
+        nc.scalar.copy(h[0][:, fourth], product(0, fourth, "acc0_2")[:])
         nc.scalar.copy(h[1][:, vertex_halves[1]], product(1, vertex_halves[1], "acc1_1")[:])
         accs = {t: product(t, slice(0, S), "acc%d" % t) for t in pairs[1]}
         for cols in vertex_halves:

@@ -138,20 +138,22 @@ def tile_picked_ypm_pm_po_kernel(
                     nc.vector.tensor_tensor(d[t][:, i, :], h[t][:].indirect(pos_t[i][:]), hc[:, t, :], ALU.subtract)
 
         even_then_y = sb.tile([P, PACK, V], F32, name="work", tag="words_then_codes", align_bytes=64)
-        odd_then_part = sb.tile([P, 3 * V], F32, name="work", tag="w_scales1", align_bytes=64)
-        work_even = even_then_y[:, 0:2, :]
+        odd_then_part = sb.tile([P, 4 * V], F32, name="work", tag="w_scales1", align_bytes=64)
+        work_even = even_then_y[:, 1:3, :]
         work_odd = odd_then_part[:, 0 : 2 * V].rearrange("p (i v) -> p i v", i=2)
-        work = [work_even, work_odd]
+        lap = 32
+        work_first_odd = odd_then_part[:, lap : lap + 2 * V].rearrange("p (i v) -> p i v", i=2)
+        work = [work_even, work_first_odd, work_even, work_odd]
         both = slice(0, 2)
 
         def square(t, i):
-            nc.scalar.activation(work[t % 2][:, i, :], d[t][:, i, :], ACT.Square)
+            nc.scalar.activation(work[t][:, i, :], d[t][:, i, :], ACT.Square)
 
         def root(t, i):
-            nc.scalar.activation(work[t % 2][:, i, :], work[t % 2][:, i, :], ACT.Abs_reciprocal_sqrt, bias=one[:])
+            nc.scalar.activation(work[t][:, i, :], work[t][:, i, :], ACT.Abs_reciprocal_sqrt, bias=one[:])
 
         def damping(t, i):
-            nc.scalar.activation(damp[t][:, i, :], work[t % 2][:, i, :], ACT.Square)
+            nc.scalar.activation(damp[t][:, i, :], work[t][:, i, :], ACT.Square)
 
         square(0, 0)
         square(0, 1)
@@ -185,13 +187,15 @@ def tile_picked_ypm_pm_po_kernel(
         y_dst = y_bf[:].rearrange("p (c r) t -> p c t r", r=run)
 
         pull(0, both)
-        for i in range(2):
-            pull(1, i)
-        part01 = sb.tile([P, 2, V], F32, name="part01")
-        nc.vector.tensor_tensor(part01[:], g[:, 0:2, 0, :], hc[:, 0:2, :], ALU.add)
-        pull(2, both)
+        part01 = odd_then_part[:, 2 * V : 4 * V].rearrange("p (t v) -> p t v", t=2)
+        pull(1, 0)
+        nc.vector.tensor_tensor(part01[:, 0, :], g[:, 0, 0, :], hc[:, 0, :], ALU.add)
+        pull(1, 1)
+        nc.vector.tensor_tensor(part01[:, 1, :], g[:, 1, 0, :], hc[:, 1, :], ALU.add)
         y = even_then_y
-        nc.vector.tensor_tensor(y[:, 0:2, :], g[:, 0:2, 1, :], part01[:], ALU.add)
+        nc.vector.tensor_tensor(y[:, 0, :], g[:, 0, 1, :], part01[:, 0, :], ALU.add)
+        pull(2, both)
+        nc.vector.tensor_tensor(y[:, 1, :], g[:, 1, 1, :], part01[:, 1, :], ALU.add)
         nc.sync.dma_start(out_rows[:, 0:2, :], y[:, 0:2, :])
 
         for i in range(2):

@@ -45,12 +45,12 @@ def tile_picked_ypm_pm_po_kernel(
         one = sb.tile([P, 1], F32, name="one")
 
         nc.scalar.dma_start(x_scales_all[SCALE_ROWS:QUADRANT, :].bitcast(I32), x_scales[0].bitcast(I32))
+        nc.gpsimd.memset(one_in[:], 1.0)
         nc.gpsimd.memset(x_scales_all[0:SCALE_ROWS, :].bitcast(I32), 0)
         for rows in (slice(QUADRANT, 2 * QUADRANT), slice(2 * QUADRANT, P)):
-            nc.vector.memset(x_scales_all[rows, :].bitcast(I32), 0)
+            nc.gpsimd.memset(x_scales_all[rows, :].bitcast(I32), 0)
         x_scales_placed = sb.tile([P, S], U8, name="x_scales_placed", align_bytes=64)
         nc.gpsimd.memset(x_scales_placed[:].bitcast(I32), 0)
-        nc.vector.memset(one_in[:], 1.0)
         nc.scalar.activation(one[:], one_in[:], ACT.Abs_reciprocal_sqrt)
 
         w_rows = w1.rearrange("(p j) n -> p j n", j=PACK)

@@ -122,9 +122,8 @@ def tile_picked_ypm_pm_po_kernel(
         nc.scalar.copy(h[0][:, fourth], product(0, fourth, "acc0_2")[:])
         nc.scalar.copy(h[1][:, vertex_halves[1]], product(1, vertex_halves[1], "acc1_1")[:])
         accs = {t: product(t, slice(0, S), "acc%d" % t) for t in pairs[1]}
-        for cols in vertex_halves:
-            for t in pairs[1]:
-                nc.scalar.copy(h[t][:, cols], accs[t][:, cols])
+        for t in pairs[1]:
+            nc.scalar.copy(h[t][:], accs[t][:])
 
         hc = sb.tile([P, PACK, V], F32, name="hc")
         d = [sb.tile([P, 2, V], F32, name="d%d" % t) for t in range(PACK)]

@@ -221,7 +221,7 @@ def tile_picked_ypm_pm_po_kernel(
             )
             nc.sync.dma_start(out_words[:, cols], y_codes[:, cols].bitcast(I32))
         for r in range(QUADRANT_ROWS):
-            queue = nc.scalar if r == 0 else nc.sync
+            queue = nc.scalar if r < QUADRANT_ROWS // 2 else nc.sync
             queue.dma_start(
                 out_2[0, r:SCALE_ROWS:QUADRANT_ROWS, :].bitcast(I32), y_scales[r:P:QUADRANT, :].bitcast(I32)
             )

@@ -113,61 +113,66 @@ def tile_picked_ypm_pm_po_kernel(
             return acc
 
         h = [sb.tile([P, S], F32, name="h%d" % t) for t in range(PACK)]
-        vertex_halves = [slice(0, HALF), slice(HALF, S)]
-        pairs = [(0, 1), (2, 3)]
-        for t in pairs[0]:
-            nc.scalar.copy(h[t][:, vertex_halves[0]], product(t, vertex_halves[0], "acc%d_0" % t)[:])
-        third, fourth = slice(HALF, HALF + P), slice(HALF + P, S)
-        nc.vector.tensor_copy(h[0][:, third], product(0, third, "acc0_1")[:])
-        nc.scalar.copy(h[0][:, fourth], product(0, fourth, "acc0_2")[:])
-        nc.scalar.copy(h[1][:, vertex_halves[1]], product(1, vertex_halves[1], "acc1_1")[:])
-        accs = {t: product(t, slice(0, S), "acc%d" % t) for t in pairs[1]}
-        for t in pairs[1]:
-            nc.scalar.copy(h[t][:], accs[t][:])
-
         hc = sb.tile([P, PACK, V], F32, name="hc")
         d = [sb.tile([P, 2, V], F32, name="d%d" % t) for t in range(PACK)]
         damp = [sb.tile([P, 2, V], F32, name="damp%d" % t) for t in range(PACK)]
         g = sb.tile([P, PACK, 2, V], F32, name="g")
-        for pair in pairs:
-            for t in pair:
-                nc.vector.tensor_copy(hc[:, t, :], h[t][:].indirect(cen_t[:]))
-            for t in pair:
-                for i in range(2):
-                    nc.vector.tensor_tensor(d[t][:, i, :], h[t][:].indirect(pos_t[i][:]), hc[:, t, :], ALU.subtract)
+        first, second = slice(0, HALF), slice(HALF, S)
+        third, fourth = slice(HALF, HALF + P), slice(HALF + P, S)
 
-        even_then_y = sb.tile([P, PACK, V], F32, name="work", tag="words_then_codes", align_bytes=64)
-        odd_then_part = sb.tile([P, 4 * V], F32, name="work", tag="w_scales1", align_bytes=64)
-        work_even = even_then_y[:, 1:3, :]
-        work_odd = odd_then_part[:, 0 : 2 * V].rearrange("p (i v) -> p i v", i=2)
-        lap = 32
-        work_first_odd = odd_then_part[:, lap : lap + 2 * V].rearrange("p (i v) -> p i v", i=2)
-        work = [work_even, work_first_odd, work_even, work_odd]
+        def difference(t, i):
+            nc.vector.tensor_tensor(d[t][:, i, :], h[t][:].indirect(pos_t[i][:]), hc[:, t, :], ALU.subtract)
+
+        for t in range(2):
+            nc.scalar.copy(h[t][:, first], product(t, first, "acc%d_0" % t)[:])
+        nc.vector.tensor_copy(h[0][:, third], product(0, third, "acc0_1")[:])
+        nc.scalar.copy(h[0][:, fourth], product(0, fourth, "acc0_2")[:])
+        nc.scalar.copy(h[1][:, second], product(1, second, "acc1_1")[:])
+        accs = {t: product(t, slice(0, S), "acc%d" % t) for t in (2, 3)}
+        for t in (2, 3):
+            nc.scalar.copy(h[t][:], accs[t][:])
+        for t in range(2):
+            nc.vector.tensor_copy(hc[:, t, :], h[t][:].indirect(cen_t[:]))
+        nc.scalar.activation(hc[:, 2, :], h[2][:].indirect(cen_t[:]), ACT.Copy)
+        for t in range(3):
+            for i in range(2):
+                difference(t, i)
+
+        work = sb.tile([P, 8 * V], F32, name="work", tag="words_then_codes", align_bytes=64)
+        roots = sb.tile([P, PACK, 2, V], F32, name="roots")
+        areas = work[:, 0 : 4 * V].rearrange("p (a i v) -> p a i v", a=2, i=2)
+        squares = [areas[:, 0], areas[:, 1], areas[:, :, 0, :], areas[:, :, 0, :]]
         both = slice(0, 2)
+        last_root = sb.tile([P, V], F32, name="last_root", tag="root_then_rounded", align_bytes=64)
+
+        def root_at(t, i):
+            return last_root[:] if (t, i) == (3, 1) else roots[:, t, i, :]
 
         def square(t, i):
-            nc.scalar.activation(work[t][:, i, :], d[t][:, i, :], ACT.Square)
+            nc.scalar.activation(squares[t][:, i, :], d[t][:, i, :], ACT.Square)
 
         def root(t, i):
-            nc.scalar.activation(work[t][:, i, :], work[t][:, i, :], ACT.Abs_reciprocal_sqrt, bias=one[:])
+            nc.scalar.activation(root_at(t, i), squares[t][:, i, :], ACT.Abs_reciprocal_sqrt, bias=one[:])
 
         def damping(t, i):
-            nc.scalar.activation(damp[t][:, i, :], work[t][:, i, :], ACT.Square)
+            nc.scalar.activation(damp[t][:, i, :], root_at(t, i), ACT.Square)
 
-        square(0, 0)
-        square(0, 1)
-        square(1, 0)
+        square(0, both)
+        nc.scalar.activation(hc[:, 3, :], h[3][:].indirect(cen_t[:]), ACT.Copy)
+        for i in range(2):
+            difference(3, i)
         root(0, both)
-        square(1, 1)
+        square(1, both)
         damping(0, both)
         root(1, both)
         square(2, 0)
         damping(1, both)
         square(2, 1)
+        root(2, 0)
+        root(2, 1)
         square(3, 0)
-        root(2, both)
-        square(3, 1)
         damping(2, both)
+        square(3, 1)
         for i in range(2):
             root(3, i)
         for i in range(2):
@@ -180,36 +185,45 @@ def tile_picked_ypm_pm_po_kernel(
                 g[:, t, i, :], d[t][:, i, :], rate_t[:, t : t + 1], damp[t][:, i, :], ALU.mult, ALU.mult
             )
 
+        part1 = sb.tile([P, V], F32, name="part1")
+        part = [roots[:, 1, 0, :], part1[:], roots[:, 0, 0, :], roots[:, 0, 1, :]]
+        y = [roots[:, 1, 1, :], roots[:, 2, 0, :], roots[:, 3, 0, :], roots[:, 3, 1, :]]
+
+        def first_sum(t, cols):
+            nc.vector.tensor_tensor(part[t][:, cols], g[:, t, 0, cols], hc[:, t, cols], ALU.add)
+
+        def second_sum(t, cols):
+            nc.vector.tensor_tensor(y[t][:, cols], g[:, t, 1, cols], part[t][:, cols], ALU.add)
+
+        whole = slice(0, V)
         centre_halves = [slice(0, V // 2), slice(V // 2, V)]
-        y_bf = sb.tile([P, V, PACK], BF16, name="y_bf", align_bytes=64)
+        pull(0, both)
+        pull(1, both)
+        first_sum(0, whole)
+        first_sum(1, whole)
+        second_sum(0, whole)
+        pull(2, both)
+        second_sum(1, whole)
+        y01 = roots[:].rearrange("p t i v -> p (t i) v")[:, 3:5, :]
+        nc.sync.dma_start(out_rows[:, 0:2, :], y01)
+        first_sum(2, whole)
+        pull(3, 0)
+        second_sum(2, whole)
+        nc.sync.dma_start(out_rows[:, 2, :], y[2])
+        first_sum(3, whole)
+        pull(3, 1)
+        for cols in centre_halves:
+            second_sum(3, cols)
+        nc.sync.dma_start(out_rows[:, 3, :], y[3])
+
+        y_bf = sb.tile([P, V, PACK], BF16, name="y_bf", tag="root_then_rounded", align_bytes=64)
         run = 4
         y_dst = y_bf[:].rearrange("p (c r) t -> p c t r", r=run)
-
-        pull(0, both)
-        part01 = odd_then_part[:, 2 * V : 4 * V].rearrange("p (t v) -> p t v", t=2)
-        pull(1, 0)
-        nc.vector.tensor_tensor(part01[:, 0, :], g[:, 0, 0, :], hc[:, 0, :], ALU.add)
-        pull(1, 1)
-        nc.vector.tensor_tensor(part01[:, 1, :], g[:, 1, 0, :], hc[:, 1, :], ALU.add)
-        y = even_then_y
-        nc.vector.tensor_tensor(y[:, 0, :], g[:, 0, 1, :], part01[:, 0, :], ALU.add)
-        pull(2, both)
-        nc.vector.tensor_tensor(y[:, 1, :], g[:, 1, 1, :], part01[:, 1, :], ALU.add)
-        nc.sync.dma_start(out_rows[:, 0:2, :], y[:, 0:2, :])
-
-        for i in range(2):
-            pull(3, i)
-        part23 = odd_then_part[:, V : 3 * V].rearrange("p (t v) -> p t v", t=2)
-        for cols in centre_halves:
-            nc.vector.tensor_tensor(part23[:, :, cols], g[:, 2:4, 0, cols], hc[:, 2:4, cols], ALU.add)
-        for cols in centre_halves:
-            nc.vector.tensor_tensor(y[:, 2:4, cols], g[:, 2:4, 1, cols], part23[:, :, cols], ALU.add)
-        nc.sync.dma_start(out_rows[:, 2:4, :], y[:, 2:4, :])
-        y_src = y[:].rearrange("p t (c r) -> p c t r", r=run)
-        quarter = V // 4 // run
-        nc.scalar.copy(y_dst[:, quarter : 2 * quarter], y_src[:, quarter : 2 * quarter])
-        nc.vector.tensor_copy(y_dst[:, 0:quarter], y_src[:, 0:quarter])
-        nc.vector.tensor_copy(y_dst[:, 2 * quarter :], y_src[:, 2 * quarter :])
+        nc.scalar.copy(y_dst[:, :, 0:2], y01.rearrange("p t (c r) -> p c t r", r=run))
+        src23 = roots[:, 3].rearrange("p t (c r) -> p c t r", r=run)
+        half_runs = V // 2 // run
+        nc.scalar.copy(y_dst[:, 0:half_runs, 2:4], src23[:, 0:half_runs])
+        nc.vector.tensor_copy(y_dst[:, half_runs:, 2:4], src23[:, half_runs:])
         out_words = out_1[0].rearrange("p c r -> p (c r)").bitcast(I32)
         y_codes = sb.tile([P, V], U32, name="y_codes", align_bytes=64)
         y_scales = sb.tile([P, V], U8, name="y_scales", align_bytes=64)

@@ -113,66 +113,68 @@ def tile_picked_ypm_pm_po_kernel(
             return acc
 
         h = [sb.tile([P, S], F32, name="h%d" % t) for t in range(PACK)]
+        vertex_halves = [slice(0, HALF), slice(HALF, S)]
+        pairs = [(0, 1), (2, 3)]
+        for t in pairs[0]:
+            nc.scalar.copy(h[t][:, vertex_halves[0]], product(t, vertex_halves[0], "acc%d_0" % t)[:])
+        third, fourth = slice(HALF, HALF + P), slice(HALF + P, S)
+        nc.vector.tensor_copy(h[0][:, third], product(0, third, "acc0_1")[:])
+        nc.scalar.copy(h[0][:, fourth], product(0, fourth, "acc0_2")[:])
+        nc.scalar.copy(h[1][:, vertex_halves[1]], product(1, vertex_halves[1], "acc1_1")[:])
+        accs = {t: product(t, slice(0, S), "acc%d" % t) for t in pairs[1]}
+        for t in pairs[1]:
+            nc.scalar.copy(h[t][:], accs[t][:])
+
         hc = sb.tile([P, PACK, V], F32, name="hc")
         d = [sb.tile([P, 2, V], F32, name="d%d" % t) for t in range(PACK)]
         damp = [sb.tile([P, 2, V], F32, name="damp%d" % t) for t in range(PACK)]
         g = sb.tile([P, PACK, 2, V], F32, name="g")
-        first, second = slice(0, HALF), slice(HALF, S)
-        third, fourth = slice(HALF, HALF + P), slice(HALF + P, S)
-
         def difference(t, i):
             nc.vector.tensor_tensor(d[t][:, i, :], h[t][:].indirect(pos_t[i][:]), hc[:, t, :], ALU.subtract)
 
-        for t in range(2):
-            nc.scalar.copy(h[t][:, first], product(t, first, "acc%d_0" % t)[:])
-        nc.vector.tensor_copy(h[0][:, third], product(0, third, "acc0_1")[:])
-        nc.scalar.copy(h[0][:, fourth], product(0, fourth, "acc0_2")[:])
-        nc.scalar.copy(h[1][:, second], product(1, second, "acc1_1")[:])
-        accs = {t: product(t, slice(0, S), "acc%d" % t) for t in (2, 3)}
-        for t in (2, 3):
-            nc.scalar.copy(h[t][:], accs[t][:])
-        for t in range(2):
+        for t in pairs[0]:
             nc.vector.tensor_copy(hc[:, t, :], h[t][:].indirect(cen_t[:]))
         nc.scalar.activation(hc[:, 2, :], h[2][:].indirect(cen_t[:]), ACT.Copy)
-        for t in range(3):
+        for t in pairs[0]:
             for i in range(2):
                 difference(t, i)
-
-        work = sb.tile([P, 8 * V], F32, name="work", tag="words_then_codes", align_bytes=64)
-        roots = sb.tile([P, PACK, 2, V], F32, name="roots")
-        areas = work[:, 0 : 4 * V].rearrange("p (a i v) -> p a i v", a=2, i=2)
-        squares = [areas[:, 0], areas[:, 1], areas[:, :, 0, :], areas[:, :, 0, :]]
-        both = slice(0, 2)
-        last_root = sb.tile([P, V], F32, name="last_root", tag="root_then_rounded", align_bytes=64)
-
-        def root_at(t, i):
-            return last_root[:] if (t, i) == (3, 1) else roots[:, t, i, :]
-
-        def square(t, i):
-            nc.scalar.activation(squares[t][:, i, :], d[t][:, i, :], ACT.Square)
-
-        def root(t, i):
-            nc.scalar.activation(root_at(t, i), squares[t][:, i, :], ACT.Abs_reciprocal_sqrt, bias=one[:])
-
-        def damping(t, i):
-            nc.scalar.activation(damp[t][:, i, :], root_at(t, i), ACT.Square)
-
-        square(0, both)
-        nc.scalar.activation(hc[:, 3, :], h[3][:].indirect(cen_t[:]), ACT.Copy)
+        difference(2, 0)
+        nc.vector.tensor_copy(hc[:, 3, :], h[3][:].indirect(cen_t[:]))
+        difference(2, 1)
         for i in range(2):
             difference(3, i)
+
+        even_then_y = sb.tile([P, PACK, V], F32, name="work", tag="words_then_codes", align_bytes=64)
+        odd_then_part = sb.tile([P, 4 * V], F32, name="work", tag="w_scales1", align_bytes=64)
+        work_even = even_then_y[:, 1:3, :]
+        work_odd = odd_then_part[:, 0 : 2 * V].rearrange("p (i v) -> p i v", i=2)
+        lap = 32
+        work_first_odd = odd_then_part[:, lap : lap + 2 * V].rearrange("p (i v) -> p i v", i=2)
+        work = [work_even, work_first_odd, work_even, work_odd]
+        both = slice(0, 2)
+
+        def square(t, i):
+            nc.scalar.activation(work[t][:, i, :], d[t][:, i, :], ACT.Square)
+
+        def root(t, i):
+            nc.scalar.activation(work[t][:, i, :], work[t][:, i, :], ACT.Abs_reciprocal_sqrt, bias=one[:])
+
+        def damping(t, i):
+            nc.scalar.activation(damp[t][:, i, :], work[t][:, i, :], ACT.Square)
+
+        square(0, both)
+        square(1, 0)
         root(0, both)
-        square(1, both)
+        square(1, 1)
         damping(0, both)
         root(1, both)
         square(2, 0)
         damping(1, both)
         square(2, 1)
-        root(2, 0)
-        root(2, 1)
         square(3, 0)
-        damping(2, both)
+        root(2, both)
         square(3, 1)
+        damping(2, both)
         for i in range(2):
             root(3, i)
         for i in range(2):
@@ -185,45 +187,36 @@ def tile_picked_ypm_pm_po_kernel(
                 g[:, t, i, :], d[t][:, i, :], rate_t[:, t : t + 1], damp[t][:, i, :], ALU.mult, ALU.mult
             )
 
-        part1 = sb.tile([P, V], F32, name="part1")
-        part = [roots[:, 1, 0, :], part1[:], roots[:, 0, 0, :], roots[:, 0, 1, :]]
-        y = [roots[:, 1, 1, :], roots[:, 2, 0, :], roots[:, 3, 0, :], roots[:, 3, 1, :]]
-
-        def first_sum(t, cols):
-            nc.vector.tensor_tensor(part[t][:, cols], g[:, t, 0, cols], hc[:, t, cols], ALU.add)
-
-        def second_sum(t, cols):
-            nc.vector.tensor_tensor(y[t][:, cols], g[:, t, 1, cols], part[t][:, cols], ALU.add)
-
-        whole = slice(0, V)
         centre_halves = [slice(0, V // 2), slice(V // 2, V)]
-        pull(0, both)
-        pull(1, both)
-        first_sum(0, whole)
-        first_sum(1, whole)
-        second_sum(0, whole)
-        pull(2, both)
-        second_sum(1, whole)
-        y01 = roots[:].rearrange("p t i v -> p (t i) v")[:, 3:5, :]
-        nc.sync.dma_start(out_rows[:, 0:2, :], y01)
-        first_sum(2, whole)
-        pull(3, 0)
-        second_sum(2, whole)
-        nc.sync.dma_start(out_rows[:, 2, :], y[2])
-        first_sum(3, whole)
-        pull(3, 1)
-        for cols in centre_halves:
-            second_sum(3, cols)
-        nc.sync.dma_start(out_rows[:, 3, :], y[3])
-
-        y_bf = sb.tile([P, V, PACK], BF16, name="y_bf", tag="root_then_rounded", align_bytes=64)
+        y_bf = sb.tile([P, V, PACK], BF16, name="y_bf", align_bytes=64)
         run = 4
         y_dst = y_bf[:].rearrange("p (c r) t -> p c t r", r=run)
-        nc.scalar.copy(y_dst[:, :, 0:2], y01.rearrange("p t (c r) -> p c t r", r=run))
-        src23 = roots[:, 3].rearrange("p t (c r) -> p c t r", r=run)
-        half_runs = V // 2 // run
-        nc.scalar.copy(y_dst[:, 0:half_runs, 2:4], src23[:, 0:half_runs])
-        nc.vector.tensor_copy(y_dst[:, half_runs:, 2:4], src23[:, half_runs:])
+
+        pull(0, both)
+        part01 = odd_then_part[:, 2 * V : 4 * V].rearrange("p (t v) -> p t v", t=2)
+        pull(1, 0)
+        nc.vector.tensor_tensor(part01[:, 0, :], g[:, 0, 0, :], hc[:, 0, :], ALU.add)
+        pull(1, 1)
+        nc.vector.tensor_tensor(part01[:, 1, :], g[:, 1, 0, :], hc[:, 1, :], ALU.add)
+        y = even_then_y
+        nc.vector.tensor_tensor(y[:, 0, :], g[:, 0, 1, :], part01[:, 0, :], ALU.add)
+        pull(2, both)
+        nc.vector.tensor_tensor(y[:, 1, :], g[:, 1, 1, :], part01[:, 1, :], ALU.add)
+        nc.sync.dma_start(out_rows[:, 0:2, :], y[:, 0:2, :])
+
+        for i in range(2):
+            pull(3, i)
+        part23 = odd_then_part[:, V : 3 * V].rearrange("p (t v) -> p t v", t=2)
+        for cols in centre_halves:
+            nc.vector.tensor_tensor(part23[:, :, cols], g[:, 2:4, 0, cols], hc[:, 2:4, cols], ALU.add)
+        for cols in centre_halves:
+            nc.vector.tensor_tensor(y[:, 2:4, cols], g[:, 2:4, 1, cols], part23[:, :, cols], ALU.add)
+        nc.sync.dma_start(out_rows[:, 2:4, :], y[:, 2:4, :])
+        y_src = y[:].rearrange("p t (c r) -> p c t r", r=run)
+        quarter = V // 4 // run
+        nc.scalar.copy(y_dst[:, quarter : 2 * quarter], y_src[:, quarter : 2 * quarter])
+        nc.vector.tensor_copy(y_dst[:, 0:quarter], y_src[:, 0:quarter])
+        nc.vector.tensor_copy(y_dst[:, 2 * quarter :], y_src[:, 2 * quarter :])
         out_words = out_1[0].rearrange("p c r -> p (c r)").bitcast(I32)
         y_codes = sb.tile([P, V], U32, name="y_codes", align_bytes=64)
         y_scales = sb.tile([P, V], U8, name="y_scales", align_bytes=64)

@@ -150,24 +150,25 @@ def tile_picked_ypm_pm_po_kernel(
         work_odd = odd_then_part[:, 0 : 2 * V].rearrange("p (i v) -> p i v", i=2)
         lap = 32
         work_first_odd = odd_then_part[:, lap : lap + 2 * V].rearrange("p (i v) -> p i v", i=2)
-        work = [work_even, work_first_odd, work_even, work_odd]
+        squares = [even_then_y[:, 0:PACK:3, :], work_even, work_even, work_odd]
+        roots = [damp[0][:], work_first_odd, work_even, work_odd]
         both = slice(0, 2)
 
         def square(t, i):
-            nc.scalar.activation(work[t][:, i, :], d[t][:, i, :], ACT.Square)
+            nc.scalar.activation(squares[t][:, i, :], d[t][:, i, :], ACT.Square)
 
         def root(t, i):
-            nc.scalar.activation(work[t][:, i, :], work[t][:, i, :], ACT.Abs_reciprocal_sqrt, bias=one[:])
+            nc.scalar.activation(roots[t][:, i, :], squares[t][:, i, :], ACT.Abs_reciprocal_sqrt, bias=one[:])
 
         def damping(t, i):
-            nc.scalar.activation(damp[t][:, i, :], work[t][:, i, :], ACT.Square)
+            nc.scalar.activation(damp[t][:, i, :], roots[t][:, i, :], ACT.Square)
 
         square(0, both)
         square(1, 0)
         root(0, both)
         square(1, 1)
-        damping(0, both)
-        root(1, both)
+        root(1, 0)
+        root(1, 1)
         square(2, 0)
         damping(1, both)
         square(2, 1)
@@ -193,13 +194,15 @@ def tile_picked_ypm_pm_po_kernel(
         y_dst = y_bf[:].rearrange("p (c r) t -> p c t r", r=run)
 
         pull(0, both)
-        part01 = odd_then_part[:, 2 * V : 4 * V].rearrange("p (t v) -> p t v", t=2)
+        g0 = odd_then_part[:, 2 * V : 4 * V].rearrange("p (i v) -> p i v", i=2)
+        part01 = sb.tile([P, 2, V], F32, name="part01")
         pull(1, 0)
-        nc.vector.tensor_tensor(part01[:, 0, :], g[:, 0, 0, :], hc[:, 0, :], ALU.add)
+        nc.vector.tensor_tensor(g0, g[:, 0], roots[0], ALU.mult)
         pull(1, 1)
+        nc.vector.tensor_tensor(part01[:, 0, :], g0[:, 0, :], hc[:, 0, :], ALU.add)
         nc.vector.tensor_tensor(part01[:, 1, :], g[:, 1, 0, :], hc[:, 1, :], ALU.add)
         y = even_then_y
-        nc.vector.tensor_tensor(y[:, 0, :], g[:, 0, 1, :], part01[:, 0, :], ALU.add)
+        nc.vector.tensor_tensor(y[:, 0, :], g0[:, 1, :], part01[:, 0, :], ALU.add)
         pull(2, both)
         nc.vector.tensor_tensor(y[:, 1, :], g[:, 1, 1, :], part01[:, 1, :], ALU.add)
         nc.sync.dma_start(out_rows[:, 0:2, :], y[:, 0:2, :])

@@ -1,6 +1,7 @@
 from contextlib import ExitStack
 
 import concourse.mybir as mybir
+from concourse.masks import make_identity
 
 K, T, S, V, N = 512, 2048, 512, 256, 512
 FLOPS = 2 * K * S * N
@@ -51,6 +52,8 @@ def tile_picked_ypm_pm_po_kernel(
             nc.gpsimd.memset(x_scales_all[rows, :].bitcast(I32), 0)
         x_scales_placed = sb.tile([P, S], U8, name="x_scales_placed", align_bytes=64)
         nc.gpsimd.memset(x_scales_placed[:].bitcast(I32), 0)
+        identity = sb.tile([P, P], F32, name="identity")
+        make_identity(nc, identity[:])
         nc.scalar.activation(one[:], one_in[:], ACT.Abs_reciprocal_sqrt)
 
         w_rows = w1.rearrange("(p j) n -> p j n", j=PACK)
@@ -134,52 +137,66 @@ def tile_picked_ypm_pm_po_kernel(
 
         for t in pairs[0]:
             nc.vector.tensor_copy(hc[:, t, :], h[t][:].indirect(cen_t[:]))
-        nc.scalar.activation(hc[:, 2, :], h[2][:].indirect(cen_t[:]), ACT.Copy)
-        for t in pairs[0]:
+        for t in pairs[1]:
+            nc.scalar.activation(hc[:, t, :], h[t][:].indirect(cen_t[:]), ACT.Copy)
+        for t in range(PACK):
             for i in range(2):
                 difference(t, i)
-        difference(2, 0)
-        nc.vector.tensor_copy(hc[:, 3, :], h[3][:].indirect(cen_t[:]))
-        difference(2, 1)
-        for i in range(2):
-            difference(3, i)
 
-        even_then_y = sb.tile([P, PACK, V], F32, name="work", tag="words_then_codes", align_bytes=64)
+        def turn(t, i, tag):
+            turned = psum.tile([P, 2, P], F32, name="turned", tag=tag)
+            for half in range(2):
+                nc.tensor.transpose(turned[:, half, :], d[t][:, i, half * P : (half + 1) * P], identity[:])
+            return turned[:].rearrange("p a f -> p (a f)")
+
+        d_turned = {(0, 0): turn(0, 0, "turned"), (0, 1): turn(0, 1, "acc0_0")}
+        d_turned[1, 0] = turn(1, 0, "acc1_0")
+        d_turned[1, 1] = turn(1, 1, "acc0_1")
+
+        work = sb.tile([P, 8 * V], F32, name="work", tag="words_then_codes", align_bytes=64)
         odd_then_part = sb.tile([P, 4 * V], F32, name="work", tag="w_scales1", align_bytes=64)
-        work_even = even_then_y[:, 1:3, :]
-        work_odd = odd_then_part[:, 0 : 2 * V].rearrange("p (i v) -> p i v", i=2)
+        last_squares = sb.tile([P, 2, V], F32, name="last_squares")
         lap = 32
-        work_first_odd = odd_then_part[:, lap : lap + 2 * V].rearrange("p (i v) -> p i v", i=2)
-        squares = [even_then_y[:, 0:PACK:3, :], work_even, work_even, work_odd]
-        roots = [damp[0][:], work_first_odd, work_even, work_odd]
         both = slice(0, 2)
 
+        def at(start):
+            return work[:, start : start + V]
+
+        y = work[:, 4 * V : 8 * V].rearrange("p (t v) -> p t v", t=PACK)
+        root1 = odd_then_part[:, lap : lap + 2 * V].rearrange("p (i v) -> p i v", i=2)
+        squares = {(0, 0): y[:, 2, :], (0, 1): y[:, 3, :], (3, 0): last_squares[:, 0, :], (3, 1): last_squares[:, 1, :]}
+        for t in (1, 2):
+            squares[t, 0], squares[t, 1] = at(320), at(576)
+        roots = {(1, 0): root1[:, 0, :], (1, 1): root1[:, 1, :], (2, 0): at(0), (2, 1): y[:, 1, :]}
+        roots[0, 0], roots[0, 1] = damp[0][:, 0, :], damp[0][:, 1, :]
+        roots[3, 0], roots[3, 1] = at(344), at(800)
+
         def square(t, i):
-            nc.scalar.activation(squares[t][:, i, :], d[t][:, i, :], ACT.Square)
+            nc.scalar.activation(squares[t, i], d_turned[t, i] if t < 2 else d[t][:, i, :], ACT.Square)
 
         def root(t, i):
-            nc.scalar.activation(roots[t][:, i, :], squares[t][:, i, :], ACT.Abs_reciprocal_sqrt, bias=one[:])
+            nc.scalar.activation(roots[t, i], squares[t, i], ACT.Abs_reciprocal_sqrt, bias=one[:])
 
         def damping(t, i):
-            nc.scalar.activation(damp[t][:, i, :], roots[t][:, i, :], ACT.Square)
+            nc.scalar.activation(damp[t][:, i, :], roots[t, i], ACT.Square)
 
-        square(0, both)
+        for i in range(2):
+            nc.gpsimd.tensor_tensor(squares[3, i], d[3][:, i, :], d[3][:, i, :], ALU.mult)
+        square(0, 0)
+        square(0, 1)
+        root0 = damp[0]
+        root(0, 0)
+        root(0, 1)
         square(1, 0)
-        root(0, both)
         square(1, 1)
         root(1, 0)
         root(1, 1)
         square(2, 0)
-        damping(1, both)
+        nc.scalar.activation(damp[1][:], root1, ACT.Square)
         square(2, 1)
-        square(3, 0)
-        root(2, both)
-        square(3, 1)
-        damping(2, both)
-        for i in range(2):
-            root(3, i)
-        for i in range(2):
-            damping(3, i)
+        for step, t in ((root, 2), (damping, 2), (root, 3), (damping, 3)):
+            for i in range(2):
+                step(t, i)
 
         out_rows = out_0.rearrange("(p t) v -> p t v", t=PACK)
 
@@ -188,34 +205,44 @@ def tile_picked_ypm_pm_po_kernel(
                 g[:, t, i, :], d[t][:, i, :], rate_t[:, t : t + 1], damp[t][:, i, :], ALU.mult, ALU.mult
             )
 
+        def turn_back(terms, tag):
+            total = psum.tile([P, V], F32, name="total", tag=tag)
+            for half in range(2):
+                cols = slice(half * P, (half + 1) * P)
+                for i in range(2):
+                    nc.tensor.matmul(
+                        total[:, cols], terms[:, i, cols], identity[:], start=(i == 0), stop=(i == 1), is_transpose=True
+                    )
+            return total
+
+        def finish(t, total):
+            nc.vector.scalar_tensor_tensor(y[:, t, :], total[:], rate_t[:, t : t + 1], hc[:, t, :], ALU.mult, ALU.add)
+
         centre_halves = [slice(0, V // 2), slice(V // 2, V)]
         y_bf = sb.tile([P, V, PACK], BF16, name="y_bf", align_bytes=64)
         run = 4
         y_dst = y_bf[:].rearrange("p (c r) t -> p c t r", r=run)
 
-        pull(0, both)
+        for t in range(2):
+            for i in range(2):
+                nc.vector.tensor_tensor(g[:, t, i, :], d_turned[t, i], damp[t][:, i, :], ALU.mult)
+        total1 = turn_back(g[:, 1], "acc1_1")
         g0 = odd_then_part[:, 2 * V : 4 * V].rearrange("p (i v) -> p i v", i=2)
-        part01 = sb.tile([P, 2, V], F32, name="part01")
-        pull(1, 0)
-        nc.vector.tensor_tensor(g0, g[:, 0], roots[0], ALU.mult)
-        pull(1, 1)
-        nc.vector.tensor_tensor(part01[:, 0, :], g0[:, 0, :], hc[:, 0, :], ALU.add)
-        nc.vector.tensor_tensor(part01[:, 1, :], g[:, 1, 0, :], hc[:, 1, :], ALU.add)
-        y = even_then_y
-        nc.vector.tensor_tensor(y[:, 0, :], g0[:, 1, :], part01[:, 0, :], ALU.add)
+        nc.vector.tensor_tensor(g0, g[:, 0], root0[:], ALU.mult)
+        total0 = turn_back(g0, "acc0_2")
         pull(2, both)
-        nc.vector.tensor_tensor(y[:, 1, :], g[:, 1, 1, :], part01[:, 1, :], ALU.add)
+        finish(1, total1)
+        pull(3, 0)
+        pull(3, 1)
+        finish(0, total0)
         nc.sync.dma_start(out_rows[:, 0:2, :], y[:, 0:2, :])
-
-        for i in range(2):
-            pull(3, i)
-        part23 = odd_then_part[:, V : 3 * V].rearrange("p (t v) -> p t v", t=2)
+        part23 = work[:, 288 : 288 + 960].rearrange("p (t v) -> p t v", t=2)[:, :, 0:V]
         for cols in centre_halves:
             nc.vector.tensor_tensor(part23[:, :, cols], g[:, 2:4, 0, cols], hc[:, 2:4, cols], ALU.add)
         for cols in centre_halves:
             nc.vector.tensor_tensor(y[:, 2:4, cols], g[:, 2:4, 1, cols], part23[:, :, cols], ALU.add)
         nc.sync.dma_start(out_rows[:, 2:4, :], y[:, 2:4, :])
-        y_src = y[:].rearrange("p t (c r) -> p c t r", r=run)
+        y_src = y.rearrange("p t (c r) -> p c t r", r=run)
         quarter = V // 4 // run
         nc.scalar.copy(y_dst[:, quarter : 2 * quarter], y_src[:, quarter : 2 * quarter])
         nc.vector.tensor_copy(y_dst[:, 0:quarter], y_src[:, 0:quarter])

@@ -129,76 +129,60 @@ def tile_picked_ypm_pm_po_kernel(
             nc.scalar.copy(h[t][:], accs[t][:])
 
         hc = sb.tile([P, PACK, V], F32, name="hc")
-        d = [sb.tile([P, 2, V], F32, name="d%d" % t) for t in range(PACK)]
         damp = [sb.tile([P, 2, V], F32, name="damp%d" % t) for t in range(PACK)]
         g = sb.tile([P, PACK, 2, V], F32, name="g")
+        g0 = sb.tile([P, 2, V], F32, name="g0")
+        work = sb.tile([P, 8 * V], F32, name="work", tag="words_then_codes", align_bytes=64)
+
+        def area(start, count=1):
+            return work[:, start : start + count * V]
+
+        def two(ap):
+            return ap.rearrange("p (i v) -> p i v", i=2)
+
+        y = area(0, PACK).rearrange("p (t v) -> p t v", t=PACK)
+        d = [sb.tile([P, 2, V], F32, name="d%d" % t)[:] for t in range(3)] + [two(area(4 * V, 2))]
+        first, second = area(6 * V), area(2 * V + V // 2)
+        root1 = y[:, 0:2, :]
+        step = 2 * V - P // 2
+        scattered = work[:, 3 * V : 3 * V + 2 * step].rearrange("p (a x) -> p a x", a=2)[:, :, 0:P]
+        squares = {(0, 0): first, (0, 1): scattered}
+        for t in (1, 2):
+            squares[t, 0], squares[t, 1] = first, second
+        roots = {(0, i): damp[0][:, i, :] for i in range(2)}
+        roots.update({(1, i): root1[:, i, :] for i in range(2)})
+        roots[2, 0], roots[2, 1] = area(7 * V), y[:, 1, :]
+        roots[3, 0], roots[3, 1] = first, second
+
         def difference(t, i):
             nc.vector.tensor_tensor(d[t][:, i, :], h[t][:].indirect(pos_t[i][:]), hc[:, t, :], ALU.subtract)
 
-        for t in pairs[0]:
-            nc.vector.tensor_copy(hc[:, t, :], h[t][:].indirect(cen_t[:]))
-        for t in pairs[1]:
-            nc.scalar.activation(hc[:, t, :], h[t][:].indirect(cen_t[:]), ACT.Copy)
-        for t in range(PACK):
-            for i in range(2):
-                difference(t, i)
+        d_turned = {}
+        banks = {(0, 0): "turned", (0, 1): "acc0_0", (1, 0): "acc1_0", (1, 1): "acc0_1", (2, 0): "acc0_2", (2, 1): "acc1_1"}
 
-        def turn(t, i, tag):
-            turned = psum.tile([P, 2, P], F32, name="turned", tag=tag)
+        def turn(t, i):
+            turned = psum.tile([P, 2, P], F32, name="turned", tag=banks[t, i])
             for half in range(2):
                 nc.tensor.transpose(turned[:, half, :], d[t][:, i, half * P : (half + 1) * P], identity[:])
-            return turned[:].rearrange("p a f -> p (a f)")
-
-        d_turned = {(0, 0): turn(0, 0, "turned"), (0, 1): turn(0, 1, "acc0_0")}
-        d_turned[1, 0] = turn(1, 0, "acc1_0")
-        d_turned[1, 1] = turn(1, 1, "acc0_1")
-
-        work = sb.tile([P, 8 * V], F32, name="work", tag="words_then_codes", align_bytes=64)
-        odd_then_part = sb.tile([P, 4 * V], F32, name="work", tag="w_scales1", align_bytes=64)
-        last_squares = sb.tile([P, 2, V], F32, name="last_squares")
-        lap = 32
-        both = slice(0, 2)
-
-        def at(start):
-            return work[:, start : start + V]
-
-        y = work[:, 4 * V : 8 * V].rearrange("p (t v) -> p t v", t=PACK)
-        root1 = odd_then_part[:, lap : lap + 2 * V].rearrange("p (i v) -> p i v", i=2)
-        squares = {(0, 0): y[:, 2, :], (0, 1): y[:, 3, :], (3, 0): last_squares[:, 0, :], (3, 1): last_squares[:, 1, :]}
-        for t in (1, 2):
-            squares[t, 0], squares[t, 1] = at(320), at(576)
-        roots = {(1, 0): root1[:, 0, :], (1, 1): root1[:, 1, :], (2, 0): at(0), (2, 1): y[:, 1, :]}
-        roots[0, 0], roots[0, 1] = damp[0][:, 0, :], damp[0][:, 1, :]
-        roots[3, 0], roots[3, 1] = at(344), at(800)
+            d_turned[t, i] = turned[:].rearrange("p a f -> p (a f)")
 
         def square(t, i):
-            nc.scalar.activation(squares[t, i], d_turned[t, i] if t < 2 else d[t][:, i, :], ACT.Square)
+            source = d_turned[t, i]
+            if (t, i) == (0, 1):
+                source = source.rearrange("p (a f) -> p a f", a=2)
+            nc.scalar.activation(squares[t, i], source, ACT.Square)
 
         def root(t, i):
-            nc.scalar.activation(roots[t, i], squares[t, i], ACT.Abs_reciprocal_sqrt, bias=one[:])
+            target = roots[t, i]
+            if (t, i) == (0, 1):
+                target = target.rearrange("p (a f) -> p a f", a=2)
+            nc.scalar.activation(target, squares[t, i], ACT.Abs_reciprocal_sqrt, bias=one[:])
 
         def damping(t, i):
             nc.scalar.activation(damp[t][:, i, :], roots[t, i], ACT.Square)
 
-        for i in range(2):
-            nc.gpsimd.tensor_tensor(squares[3, i], d[3][:, i, :], d[3][:, i, :], ALU.mult)
-        square(0, 0)
-        square(0, 1)
-        root0 = damp[0]
-        root(0, 0)
-        root(0, 1)
-        square(1, 0)
-        square(1, 1)
-        root(1, 0)
-        root(1, 1)
-        square(2, 0)
-        nc.scalar.activation(damp[1][:], root1, ACT.Square)
-        square(2, 1)
-        for step, t in ((root, 2), (damping, 2), (root, 3), (damping, 3)):
-            for i in range(2):
-                step(t, i)
-
-        out_rows = out_0.rearrange("(p t) v -> p t v", t=PACK)
+        def pull_turned(t, i):
+            nc.vector.tensor_tensor(g[:, t, i, :], d_turned[t, i], damp[t][:, i, :], ALU.mult)
 
         def pull(t, i):
             nc.vector.scalar_tensor_tensor(
@@ -207,40 +191,74 @@ def tile_picked_ypm_pm_po_kernel(
 
         def turn_back(terms, tag):
             total = psum.tile([P, V], F32, name="total", tag=tag)
-            for half in range(2):
-                cols = slice(half * P, (half + 1) * P)
-                for i in range(2):
+            for i in range(2):
+                for half in range(2):
+                    cols = slice(half * P, (half + 1) * P)
                     nc.tensor.matmul(
-                        total[:, cols], terms[:, i, cols], identity[:], start=(i == 0), stop=(i == 1), is_transpose=True
+                        total[:, cols],
+                        terms[:, i, cols],
+                        identity[:],
+                        start=(i, half) == (0, 0),
+                        stop=(i, half) == (1, 1),
+                        is_transpose=True,
                     )
             return total
 
         def finish(t, total):
             nc.vector.scalar_tensor_tensor(y[:, t, :], total[:], rate_t[:, t : t + 1], hc[:, t, :], ALU.mult, ALU.add)
 
+        for t in pairs[0]:
+            nc.vector.tensor_copy(hc[:, t, :], h[t][:].indirect(cen_t[:]))
+        for t in pairs[1]:
+            nc.scalar.activation(hc[:, t, :], h[t][:].indirect(cen_t[:]), ACT.Copy)
+        for t in range(3):
+            for i in range(2):
+                difference(t, i)
+                turn(t, i)
+        for stage in (square, root):
+            for i in range(2):
+                stage(0, i)
+        for i in range(2):
+            pull_turned(0, i)
+        difference(3, 0)
+        nc.vector.tensor_tensor(g0[:], g[:, 0], damp[0][:], ALU.mult)
+        difference(3, 1)
+        total0 = turn_back(g0[:], "acc2")
+        last_squares = sb.tile([P, 2, V], F32, name="last_squares")
+        for i in range(2):
+            squares[3, i] = last_squares[:, i, :]
+            nc.vector.tensor_tensor(squares[3, i], d[3][:, i, :], d[3][:, i, :], ALU.mult)
+        for stage in (square, root):
+            for i in range(2):
+                stage(1, i)
+        square(2, 0)
+        nc.scalar.activation(damp[1][:], root1, ACT.Square)
+        square(2, 1)
+        for stage, t in ((root, 2), (damping, 2), (root, 3), (damping, 3)):
+            for i in range(2):
+                stage(t, i)
+
+        out_rows = out_0.rearrange("(p t) v -> p t v", t=PACK)
         centre_halves = [slice(0, V // 2), slice(V // 2, V)]
         y_bf = sb.tile([P, V, PACK], BF16, name="y_bf", align_bytes=64)
         run = 4
         y_dst = y_bf[:].rearrange("p (c r) t -> p c t r", r=run)
 
-        for t in range(2):
-            for i in range(2):
-                nc.vector.tensor_tensor(g[:, t, i, :], d_turned[t, i], damp[t][:, i, :], ALU.mult)
-        total1 = turn_back(g[:, 1], "acc1_1")
-        g0 = odd_then_part[:, 2 * V : 4 * V].rearrange("p (i v) -> p i v", i=2)
-        nc.vector.tensor_tensor(g0, g[:, 0], root0[:], ALU.mult)
-        total0 = turn_back(g0, "acc0_2")
-        pull(2, both)
+        for i in range(2):
+            pull_turned(1, i)
+        total1 = turn_back(g[:, 1], "acc3")
+        finish(0, total0)
+        for i in range(2):
+            pull_turned(2, i)
+        total2 = turn_back(g[:, 2], "turned")
         finish(1, total1)
+        nc.sync.dma_start(out_rows[:, 0:2, :], y[:, 0:2, :])
         pull(3, 0)
         pull(3, 1)
-        finish(0, total0)
-        nc.sync.dma_start(out_rows[:, 0:2, :], y[:, 0:2, :])
-        part23 = work[:, 288 : 288 + 960].rearrange("p (t v) -> p t v", t=2)[:, :, 0:V]
+        nc.vector.tensor_tensor(y[:, 3, :], g[:, 3, 0, :], hc[:, 3, :], ALU.add)
+        finish(2, total2)
         for cols in centre_halves:
-            nc.vector.tensor_tensor(part23[:, :, cols], g[:, 2:4, 0, cols], hc[:, 2:4, cols], ALU.add)
-        for cols in centre_halves:
-            nc.vector.tensor_tensor(y[:, 2:4, cols], g[:, 2:4, 1, cols], part23[:, :, cols], ALU.add)
+            nc.vector.tensor_tensor(y[:, 3, cols], g[:, 3, 1, cols], y[:, 3, cols], ALU.add)
         nc.sync.dma_start(out_rows[:, 2:4, :], y[:, 2:4, :])
         y_src = y.rearrange("p t (c r) -> p c t r", r=run)
         quarter = V // 4 // run

@@ -132,7 +132,7 @@ def tile_picked_ypm_pm_po_kernel(
         damp = [sb.tile([P, 2, V], F32, name="damp%d" % t) for t in range(PACK)]
         g = sb.tile([P, PACK, 2, V], F32, name="g")
         g0 = sb.tile([P, 2, V], F32, name="g0")
-        work = sb.tile([P, 8 * V], F32, name="work", tag="words_then_codes", align_bytes=64)
+        work = sb.tile([P, 9 * V], F32, name="work", tag="words_then_codes", align_bytes=64)
 
         def area(start, count=1):
             return work[:, start : start + count * V]
@@ -144,9 +144,9 @@ def tile_picked_ypm_pm_po_kernel(
         d = [sb.tile([P, 2, V], F32, name="d%d" % t)[:] for t in range(3)] + [two(area(4 * V, 2))]
         first, second = area(6 * V), area(2 * V + V // 2)
         root1 = y[:, 0:2, :]
-        step = 2 * V - P // 2
+        step = 3 * V
         scattered = work[:, 3 * V : 3 * V + 2 * step].rearrange("p (a x) -> p a x", a=2)[:, :, 0:P]
-        squares = {(0, 0): first, (0, 1): scattered}
+        squares = {(0, 0): scattered, (0, 1): area(4 * V + V // 2)}
         for t in (1, 2):
             squares[t, 0], squares[t, 1] = first, second
         roots = {(0, i): damp[0][:, i, :] for i in range(2)}
@@ -168,13 +168,13 @@ def tile_picked_ypm_pm_po_kernel(
 
         def square(t, i):
             source = d_turned[t, i]
-            if (t, i) == (0, 1):
+            if (t, i) == (0, 0):
                 source = source.rearrange("p (a f) -> p a f", a=2)
             nc.scalar.activation(squares[t, i], source, ACT.Square)
 
         def root(t, i):
             target = roots[t, i]
-            if (t, i) == (0, 1):
+            if (t, i) == (0, 0):
                 target = target.rearrange("p (a f) -> p a f", a=2)
             nc.scalar.activation(target, squares[t, i], ACT.Abs_reciprocal_sqrt, bias=one[:])
 
@@ -276,7 +276,7 @@ def tile_picked_ypm_pm_po_kernel(
             )
             nc.sync.dma_start(out_words[:, cols], y_codes[:, cols].bitcast(I32))
         for r in range(QUADRANT_ROWS):
-            queue = nc.scalar if r < QUADRANT_ROWS // 2 else nc.sync
+            queue = nc.scalar if r == 0 else nc.sync
             queue.dma_start(
                 out_2[0, r:SCALE_ROWS:QUADRANT_ROWS, :].bitcast(I32), y_scales[r:P:QUADRANT, :].bitcast(I32)
             )

@@ -131,8 +131,7 @@ def tile_picked_ypm_pm_po_kernel(
         hc = sb.tile([P, PACK, V], F32, name="hc")
         damp = [sb.tile([P, 2, V], F32, name="damp%d" % t) for t in range(PACK)]
         g = sb.tile([P, PACK, 2, V], F32, name="g")
-        g0 = sb.tile([P, 2, V], F32, name="g0")
-        work = sb.tile([P, 9 * V], F32, name="work", tag="words_then_codes", align_bytes=64)
+        work = sb.tile([P, 11 * V], F32, name="work", tag="words_then_codes", align_bytes=64)
 
         def area(start, count=1):
             return work[:, start : start + count * V]
@@ -140,19 +139,20 @@ def tile_picked_ypm_pm_po_kernel(
         def two(ap):
             return ap.rearrange("p (i v) -> p i v", i=2)
 
-        y = area(0, PACK).rearrange("p (t v) -> p t v", t=PACK)
-        d = [sb.tile([P, 2, V], F32, name="d%d" % t)[:] for t in range(3)] + [two(area(4 * V, 2))]
-        first, second = area(6 * V), area(2 * V + V // 2)
-        root1 = y[:, 0:2, :]
-        step = 3 * V
-        scattered = work[:, 3 * V : 3 * V + 2 * step].rearrange("p (a x) -> p a x", a=2)[:, :, 0:P]
-        squares = {(0, 0): scattered, (0, 1): area(4 * V + V // 2)}
-        for t in (1, 2):
-            squares[t, 0], squares[t, 1] = first, second
+        g0 = two(area(V, 2))
+        y = area(3 * V, PACK).rearrange("p (t v) -> p t v", t=PACK)
+        d = [sb.tile([P, 2, V], F32, name="d%d" % t)[:] for t in range(PACK)]
+        first_square3 = sb.tile([P, V], F32, name="first_square3")
+        across_y23 = area(5 * V + V // 2)
+        squares = {(0, 0): area(9 * V), (0, 1): area(10 * V), (1, 0): area(8 * V), (1, 1): across_y23}
+        squares.update({(2, 0): area(7 * V), (2, 1): y[:, 0, :], (3, 0): first_square3[:], (3, 1): area(0)})
         roots = {(0, i): damp[0][:, i, :] for i in range(2)}
-        roots.update({(1, i): root1[:, i, :] for i in range(2)})
-        roots[2, 0], roots[2, 1] = area(7 * V), y[:, 1, :]
-        roots[3, 0], roots[3, 1] = first, second
+        roots[1, 0], roots[1, 1] = two(area(3 * V, 8))[:, :, 0:P], area(V // 2)
+        roots[2, 0], roots[2, 1] = area(8 * V), y[:, 1, :]
+        roots[3, 0], roots[3, 1] = y[:, 0, :], across_y23
+
+        def like_root(ap, t, i):
+            return two(ap) if (t, i) == (1, 0) else ap
 
         def difference(t, i):
             nc.vector.tensor_tensor(d[t][:, i, :], h[t][:].indirect(pos_t[i][:]), hc[:, t, :], ALU.subtract)
@@ -167,19 +167,13 @@ def tile_picked_ypm_pm_po_kernel(
             d_turned[t, i] = turned[:].rearrange("p a f -> p (a f)")
 
         def square(t, i):
-            source = d_turned[t, i]
-            if (t, i) == (0, 0):
-                source = source.rearrange("p (a f) -> p a f", a=2)
-            nc.scalar.activation(squares[t, i], source, ACT.Square)
+            nc.scalar.activation(squares[t, i], d_turned[t, i], ACT.Square)
 
         def root(t, i):
-            target = roots[t, i]
-            if (t, i) == (0, 0):
-                target = target.rearrange("p (a f) -> p a f", a=2)
-            nc.scalar.activation(target, squares[t, i], ACT.Abs_reciprocal_sqrt, bias=one[:])
+            nc.scalar.activation(roots[t, i], like_root(squares[t, i], t, i), ACT.Abs_reciprocal_sqrt, bias=one[:])
 
         def damping(t, i):
-            nc.scalar.activation(damp[t][:, i, :], roots[t, i], ACT.Square)
+            nc.scalar.activation(like_root(damp[t][:, i, :], t, i), roots[t, i], ACT.Square)
 
         def pull_turned(t, i):
             nc.vector.tensor_tensor(g[:, t, i, :], d_turned[t, i], damp[t][:, i, :], ALU.mult)
@@ -215,26 +209,20 @@ def tile_picked_ypm_pm_po_kernel(
             for i in range(2):
                 difference(t, i)
                 turn(t, i)
-        for stage in (square, root):
-            for i in range(2):
-                stage(0, i)
         for i in range(2):
-            pull_turned(0, i)
-        difference(3, 0)
-        nc.vector.tensor_tensor(g0[:], g[:, 0], damp[0][:], ALU.mult)
-        difference(3, 1)
-        total0 = turn_back(g0[:], "acc2")
-        last_squares = sb.tile([P, 2, V], F32, name="last_squares")
-        for i in range(2):
-            squares[3, i] = last_squares[:, i, :]
-            nc.vector.tensor_tensor(squares[3, i], d[3][:, i, :], d[3][:, i, :], ALU.mult)
-        for stage in (square, root):
+            difference(3, i)
+        nc.gpsimd.tensor_tensor(squares[3, 0], d[3][:, 0, :], d[3][:, 0, :], ALU.mult)
+        for stage, t in ((square, 0), (root, 0), (square, 1), (root, 1), (damping, 1)):
             for i in range(2):
-                stage(1, i)
-        square(2, 0)
-        nc.scalar.activation(damp[1][:], root1, ACT.Square)
-        square(2, 1)
-        for stage, t in ((root, 2), (damping, 2), (root, 3), (damping, 3)):
+                stage(t, i)
+        for t in pairs[0]:
+            for i in range(2):
+                pull_turned(t, i)
+        total1 = turn_back(g[:, 1], "acc3")
+        nc.vector.tensor_tensor(g0, g[:, 0], damp[0][:], ALU.mult)
+        total0 = turn_back(g0, "acc2")
+        nc.vector.tensor_tensor(squares[3, 1], d[3][:, 1, :], d[3][:, 1, :], ALU.mult)
+        for stage, t in ((square, 2), (root, 2), (damping, 2), (root, 3), (damping, 3)):
             for i in range(2):
                 stage(t, i)
 
@@ -245,15 +233,12 @@ def tile_picked_ypm_pm_po_kernel(
         y_dst = y_bf[:].rearrange("p (c r) t -> p c t r", r=run)
 
         for i in range(2):
-            pull_turned(1, i)
-        total1 = turn_back(g[:, 1], "acc3")
-        finish(0, total0)
-        for i in range(2):
             pull_turned(2, i)
         total2 = turn_back(g[:, 2], "turned")
         finish(1, total1)
-        nc.sync.dma_start(out_rows[:, 0:2, :], y[:, 0:2, :])
         pull(3, 0)
+        finish(0, total0)
+        nc.sync.dma_start(out_rows[:, 0:2, :], y[:, 0:2, :])
         pull(3, 1)
         nc.vector.tensor_tensor(y[:, 3, :], g[:, 3, 0, :], hc[:, 3, :], ALU.add)
         finish(2, total2)

@@ -149,7 +149,7 @@ def tile_picked_ypm_pm_po_kernel(
         roots = {(0, i): damp[0][:, i, :] for i in range(2)}
         roots[1, 0], roots[1, 1] = two(area(3 * V, 8))[:, :, 0:P], area(V // 2)
         roots[2, 0], roots[2, 1] = area(8 * V), y[:, 1, :]
-        roots[3, 0], roots[3, 1] = y[:, 0, :], across_y23
+        roots[3, 0], roots[3, 1] = y[:, 0, :], y[:, 2, :]
 
         def like_root(ap, t, i):
             return two(ap) if (t, i) == (1, 0) else ap
@@ -239,8 +239,8 @@ def tile_picked_ypm_pm_po_kernel(
         pull(3, 0)
         finish(0, total0)
         nc.sync.dma_start(out_rows[:, 0:2, :], y[:, 0:2, :])
-        pull(3, 1)
         nc.vector.tensor_tensor(y[:, 3, :], g[:, 3, 0, :], hc[:, 3, :], ALU.add)
+        pull(3, 1)
         finish(2, total2)
         for cols in centre_halves:
             nc.vector.tensor_tensor(y[:, 3, cols], g[:, 3, 1, cols], y[:, 3, cols], ALU.add)

from contextlib import ExitStack

import concourse.mybir as mybir
from concourse.masks import make_identity

K, T, S, V, N = 512, 2048, 512, 256, 512
FLOPS = 2 * K * S * N

F32 = mybir.dt.float32
BF16 = mybir.dt.bfloat16
I32 = mybir.dt.int32
U32 = mybir.dt.uint32
U16 = mybir.dt.uint16
U8 = mybir.dt.uint8
FP8X4 = mybir.dt.float8_e4m3fn_x4
ACT = mybir.ActivationFunctionType
ALU = mybir.AluOpType

P = 128
PACK = 4
QUADRANT = 32
SCALE_ROWS = 16
QUADRANT_ROWS = 4
LIST_ROWS = 16
HALF = S // 2
SCALAR_CAST_COLUMNS = 96


def tile_picked_ypm_pm_po_kernel(
    tc, x_words, x_scales, w1, rate, offs, cen, pos1, pos2, out_0, out_1, out_2
):
    nc = tc.nc
    with ExitStack() as ctx:
        lists = ctx.enter_context(tc.tile_pool(name="lists", bufs=1))
        sb = ctx.enter_context(tc.tile_pool(name="sb", bufs=1))
        psum = ctx.enter_context(tc.psum_pool(name="psum", bufs=1))

        offs_t = lists.tile([P, S // LIST_ROWS], U16, name="offs_t")
        cen_t = lists.tile([P, V // LIST_ROWS], U16, name="cen_t")
        pos_t = [lists.tile([P, V // LIST_ROWS], U16, name="pos%d" % i) for i in range(2)]

        x_scales_all = sb.tile([P, T], U8, name="x_scales_all", tag="scales_then_codes", align_bytes=64)
        x_words_all = sb.tile([P, T], I32, name="x_words_all", tag="words_then_codes", align_bytes=64)
        w_raw = sb.tile([P, PACK, N], F32, name="w_raw", tag="raw_then_rate", align_bytes=64)
        one_in = sb.tile([P, 1], F32, name="one_in")
        one = sb.tile([P, 1], F32, name="one")

        nc.scalar.dma_start(x_scales_all[SCALE_ROWS:QUADRANT, :].bitcast(I32), x_scales[0].bitcast(I32))
        nc.gpsimd.memset(one_in[:], 1.0)
        nc.gpsimd.memset(x_scales_all[0:SCALE_ROWS, :].bitcast(I32), 0)
        for rows in (slice(QUADRANT, 2 * QUADRANT), slice(2 * QUADRANT, P)):
            nc.gpsimd.memset(x_scales_all[rows, :].bitcast(I32), 0)
        x_scales_placed = sb.tile([P, S], U8, name="x_scales_placed", align_bytes=64)
        nc.gpsimd.memset(x_scales_placed[:].bitcast(I32), 0)
        identity = sb.tile([P, P], F32, name="identity")
        make_identity(nc, identity[:])
        nc.scalar.activation(one[:], one_in[:], ACT.Abs_reciprocal_sqrt)

        w_rows = w1.rearrange("(p j) n -> p j n", j=PACK)
        nc.sync.dma_start(w_raw[:, 0:1, :], w_rows[:, 0:1, :])
        nc.sync.dma_start(offs_t[:], offs)
        nc.sync.dma_start(w_raw[:, 1:PACK, :], w_rows[:, 1:PACK, :])
        nc.sync.dma_start(x_words_all[:], x_words[0].rearrange("p c r -> p (c r)").bitcast(I32))
        nc.sync.dma_start(cen_t[:], cen)
        nc.sync.dma_start(pos_t[0][:], pos1)
        nc.sync.dma_start(pos_t[1][:], pos2)

        x_scales_picked = sb.tile([P, S], U8, name="x_scales_picked", align_bytes=64)
        nc.vector.tensor_copy(x_scales_picked[:], x_scales_all[:].indirect(offs_t[:]))
        for r in range(QUADRANT_ROWS):
            nc.scalar.dma_start(
                x_scales_placed[r:P:QUADRANT, :].bitcast(I32),
                x_scales_picked[SCALE_ROWS + r : QUADRANT : QUADRANT_ROWS, :].bitcast(I32),
            )

        w_bf = [sb.tile([P, 2, P, PACK], BF16, name="w_bf%d" % u, align_bytes=64) for u in range(2)]
        w_src = w_raw[:].rearrange("p j (m t) -> p m j t", t=PACK)
        w_dst = [w_bf[u][:].rearrange("p s m j -> p m j s") for u in range(2)]
        nc.scalar.copy(w_dst[0][:, 0:SCALAR_CAST_COLUMNS], w_src[:, 0:SCALAR_CAST_COLUMNS, :, 0:2])
        nc.vector.tensor_copy(w_dst[0][:, SCALAR_CAST_COLUMNS:P], w_src[:, SCALAR_CAST_COLUMNS:P, :, 0:2])
        nc.scalar.copy(w_dst[1], w_src[:, :, :, 2:4])
        rate_t = sb.tile([P, PACK], F32, name="rate_t", tag="raw_then_rate", align_bytes=64)
        nc.sync.dma_start(rate_t[:], rate.rearrange("(p t) o -> p (t o)", t=PACK))
        w_codes, w_scales = [], []

        def quantise_weights(u, tag):
            w_codes.append(sb.tile([P, 2 * P], U32, name="w_codes", tag=tag, align_bytes=64))
            w_scales.append(sb.tile([P, 2 * P], U8, name="w_scales", tag="w_scales%d" % u, align_bytes=64))
            nc.vector.quantize_mx(
                out=w_codes[u][:].bitcast(FP8X4),
                scales=w_scales[u][:],
                in_=w_bf[u][:].rearrange("p s m j -> p (s m j)"),
            )

        quantise_weights(0, "scales_then_codes")
        x_words_picked = sb.tile([P, S], U32, name="x_words_picked", align_bytes=64)
        for a in range(2):
            nc.vector.tensor_copy(
                x_words_picked[:, a * HALF : (a + 1) * HALF],
                x_words_all[:].bitcast(U32).indirect(offs_t[:, a * HALF // LIST_ROWS : (a + 1) * HALF // LIST_ROWS]),
            )
        quantise_weights(1, "words_then_codes")

        def product(t, cols, name):
            acc = psum.tile([P, cols.stop - cols.start], F32, name=name)
            tile_cols = slice(t % 2 * P, (t % 2 + 1) * P)
            nc.tensor.matmul_mx(
                out=acc[:],
                lhsT=w_codes[t // 2][:, tile_cols].bitcast(FP8X4),
                lhsT_scale=w_scales[t // 2][:, tile_cols],
                rhs=x_words_picked[:, cols].bitcast(FP8X4),
                rhs_scale=x_scales_placed[:, cols],
                start=True,
                stop=True,
            )
            return acc

        h = [sb.tile([P, S], F32, name="h%d" % t) for t in range(PACK)]
        vertex_halves = [slice(0, HALF), slice(HALF, S)]
        pairs = [(0, 1), (2, 3)]
        for t in pairs[0]:
            nc.scalar.copy(h[t][:, vertex_halves[0]], product(t, vertex_halves[0], "acc%d_0" % t)[:])
        third, fourth = slice(HALF, HALF + P), slice(HALF + P, S)
        nc.vector.tensor_copy(h[0][:, third], product(0, third, "acc0_1")[:])
        nc.scalar.copy(h[0][:, fourth], product(0, fourth, "acc0_2")[:])
        nc.scalar.copy(h[1][:, vertex_halves[1]], product(1, vertex_halves[1], "acc1_1")[:])
        accs = {t: product(t, slice(0, S), "acc%d" % t) for t in pairs[1]}
        for t in pairs[1]:
            nc.scalar.copy(h[t][:], accs[t][:])

        hc = sb.tile([P, PACK, V], F32, name="hc")
        damp = [sb.tile([P, 2, V], F32, name="damp%d" % t) for t in range(PACK)]
        g = sb.tile([P, PACK, 2, V], F32, name="g")
        work = sb.tile([P, 11 * V], F32, name="work", tag="words_then_codes", align_bytes=64)

        def area(start, count=1):
            return work[:, start : start + count * V]

        def two(ap):
            return ap.rearrange("p (i v) -> p i v", i=2)

        g0 = two(area(V, 2))
        y = area(3 * V, PACK).rearrange("p (t v) -> p t v", t=PACK)
        d = [sb.tile([P, 2, V], F32, name="d%d" % t)[:] for t in range(PACK)]
        first_square3 = sb.tile([P, V], F32, name="first_square3")
        across_y23 = area(5 * V + V // 2)
        squares = {(0, 0): area(9 * V), (0, 1): area(10 * V), (1, 0): area(8 * V), (1, 1): across_y23}
        squares.update({(2, 0): area(7 * V), (2, 1): y[:, 0, :], (3, 0): first_square3[:], (3, 1): area(0)})
        roots = {(0, i): damp[0][:, i, :] for i in range(2)}
        roots[1, 0], roots[1, 1] = two(area(3 * V, 8))[:, :, 0:P], area(V // 2)
        roots[2, 0], roots[2, 1] = area(8 * V), y[:, 1, :]
        roots[3, 0], roots[3, 1] = y[:, 0, :], y[:, 2, :]

        def like_root(ap, t, i):
            return two(ap) if (t, i) == (1, 0) else ap

        def difference(t, i):
            nc.vector.tensor_tensor(d[t][:, i, :], h[t][:].indirect(pos_t[i][:]), hc[:, t, :], ALU.subtract)

        d_turned = {}
        banks = {(0, 0): "turned", (0, 1): "acc0_0", (1, 0): "acc1_0", (1, 1): "acc0_1", (2, 0): "acc0_2", (2, 1): "acc1_1"}

        def turn(t, i):
            turned = psum.tile([P, 2, P], F32, name="turned", tag=banks[t, i])
            for half in range(2):
                nc.tensor.transpose(turned[:, half, :], d[t][:, i, half * P : (half + 1) * P], identity[:])
            d_turned[t, i] = turned[:].rearrange("p a f -> p (a f)")

        def square(t, i):
            nc.scalar.activation(squares[t, i], d_turned[t, i], ACT.Square)

        def root(t, i):
            nc.scalar.activation(roots[t, i], like_root(squares[t, i], t, i), ACT.Abs_reciprocal_sqrt, bias=one[:])

        def damping(t, i):
            nc.scalar.activation(like_root(damp[t][:, i, :], t, i), roots[t, i], ACT.Square)

        def pull_turned(t, i):
            nc.vector.tensor_tensor(g[:, t, i, :], d_turned[t, i], damp[t][:, i, :], ALU.mult)

        def pull(t, i):
            nc.vector.scalar_tensor_tensor(
                g[:, t, i, :], d[t][:, i, :], rate_t[:, t : t + 1], damp[t][:, i, :], ALU.mult, ALU.mult
            )

        def turn_back(terms, tag):
            total = psum.tile([P, V], F32, name="total", tag=tag)
            for i in range(2):
                for half in range(2):
                    cols = slice(half * P, (half + 1) * P)
                    nc.tensor.matmul(
                        total[:, cols],
                        terms[:, i, cols],
                        identity[:],
                        start=(i, half) == (0, 0),
                        stop=(i, half) == (1, 1),
                        is_transpose=True,
                    )
            return total

        def finish(t, total):
            nc.vector.scalar_tensor_tensor(y[:, t, :], total[:], rate_t[:, t : t + 1], hc[:, t, :], ALU.mult, ALU.add)

        for t in pairs[0]:
            nc.vector.tensor_copy(hc[:, t, :], h[t][:].indirect(cen_t[:]))
        for t in pairs[1]:
            nc.scalar.activation(hc[:, t, :], h[t][:].indirect(cen_t[:]), ACT.Copy)
        for t in range(3):
            for i in range(2):
                difference(t, i)
                turn(t, i)
        for i in range(2):
            difference(3, i)
        nc.gpsimd.tensor_tensor(squares[3, 0], d[3][:, 0, :], d[3][:, 0, :], ALU.mult)
        for stage, t in ((square, 0), (root, 0), (square, 1), (root, 1), (damping, 1)):
            for i in range(2):
                stage(t, i)
        for t in pairs[0]:
            for i in range(2):
                pull_turned(t, i)
        total1 = turn_back(g[:, 1], "acc3")
        nc.vector.tensor_tensor(g0, g[:, 0], damp[0][:], ALU.mult)
        total0 = turn_back(g0, "acc2")
        nc.vector.tensor_tensor(squares[3, 1], d[3][:, 1, :], d[3][:, 1, :], ALU.mult)
        for stage, t in ((square, 2), (root, 2), (damping, 2), (root, 3), (damping, 3)):
            for i in range(2):
                stage(t, i)

        out_rows = out_0.rearrange("(p t) v -> p t v", t=PACK)
        centre_halves = [slice(0, V // 2), slice(V // 2, V)]
        y_bf = sb.tile([P, V, PACK], BF16, name="y_bf", align_bytes=64)
        run = 4
        y_dst = y_bf[:].rearrange("p (c r) t -> p c t r", r=run)

        for i in range(2):
            pull_turned(2, i)
        total2 = turn_back(g[:, 2], "turned")
        finish(1, total1)
        pull(3, 0)
        finish(0, total0)
        nc.sync.dma_start(out_rows[:, 0:2, :], y[:, 0:2, :])
        nc.vector.tensor_tensor(y[:, 3, :], g[:, 3, 0, :], hc[:, 3, :], ALU.add)
        pull(3, 1)
        finish(2, total2)
        for cols in centre_halves:
            nc.vector.tensor_tensor(y[:, 3, cols], g[:, 3, 1, cols], y[:, 3, cols], ALU.add)
        nc.sync.dma_start(out_rows[:, 2:4, :], y[:, 2:4, :])
        y_src = y.rearrange("p t (c r) -> p c t r", r=run)
        quarter = V // 4 // run
        nc.scalar.copy(y_dst[:, quarter : 2 * quarter], y_src[:, quarter : 2 * quarter])
        nc.vector.tensor_copy(y_dst[:, 0:quarter], y_src[:, 0:quarter])
        nc.vector.tensor_copy(y_dst[:, 2 * quarter :], y_src[:, 2 * quarter :])
        out_words = out_1[0].rearrange("p c r -> p (c r)").bitcast(I32)
        y_codes = sb.tile([P, V], U32, name="y_codes", align_bytes=64)
        y_scales = sb.tile([P, V], U8, name="y_scales", align_bytes=64)
        for cols in centre_halves:
            nc.vector.quantize_mx(
                out=y_codes[:, cols].bitcast(FP8X4),
                scales=y_scales[:, cols],
                in_=y_bf[:, cols, :].rearrange("p v t -> p (v t)"),
            )
            nc.sync.dma_start(out_words[:, cols], y_codes[:, cols].bitcast(I32))
        for r in range(QUADRANT_ROWS):
            queue = nc.scalar if r == 0 else nc.sync
            queue.dma_start(
                out_2[0, r:SCALE_ROWS:QUADRANT_ROWS, :].bitcast(I32), y_scales[r:P:QUADRANT, :].bitcast(I32)
            )
